import numpy as np
import ml_dtypes


def mxq(x, axis, fmt="e4m3"):
    dtype, down = {"e4m3": (ml_dtypes.float8_e4m3fn, 7), "e5m2": (ml_dtypes.float8_e5m2, 14)}[fmt]
    v = np.moveaxis(np.asarray(x, np.float32).astype(ml_dtypes.bfloat16).astype(np.float64), axis, -1)
    blocks = v.reshape(v.shape[:-1] + (-1, 32))
    amax = np.abs(blocks).max(-1, keepdims=True)
    byte = np.maximum(np.where(amax > 0, np.frexp(amax)[1] - 1 + 127, 0) - down, 1)
    scale = np.exp2(byte - 127.0)
    codes = (blocks / scale).astype(np.float32).astype(dtype).astype(np.float64)
    return np.moveaxis((codes * scale).reshape(v.shape), -1, axis)


WIDE = False


def mx_kscale(k):
    if not WIDE:
        return np.ones(k)
    levels = np.array([30, -30])
    if k % 512:
        return np.exp2(np.random.permutation(np.resize(levels, k // 32))).repeat(32)
    a = np.empty((k // 512, 16))
    for p in range(k // 512):
        a[p, :8] = np.random.permutation(np.resize(levels, 8))
        for g in range(8):
            far = levels[np.abs(levels - a[p, g]) >= 10]
            a[p, g + 8] = far[np.random.randint(len(far))]
    return np.exp2(a.ravel()).repeat(32)


BF16 = ml_dtypes.bfloat16


def bf(x):
    return np.asarray(x, np.float32).astype(BF16)


def f64(x):
    return np.asarray(x).astype(np.float64)


W, R, K, M, N = 4, 1024, 4096, 512, 1024


def setup_inputs():
    s = mx_kscale(R)[None, :, None]
    burst = np.exp(0.5 * np.random.standard_normal((W, R, M)))
    u = np.random.standard_normal((W, R, M)) * burst / np.sqrt(R)
    v = np.random.standard_normal((W, R, N))
    a = np.random.uniform(0.5, 1.5, W)
    return {"u": bf(u * s),
            "v": bf(v / s),
            "a": bf(a / a.sum())}


def reference(u, v, a):
    a, u, v = f64(a)[:, None, None], f64(u), f64(v)
    au = a * u
    ubar = au.sum(axis=0)
    vbar = (a * v).sum(axis=0)
    au_q = mxq(au.reshape(K, M), 0, "e5m2")
    v_q = mxq(v.reshape(K, N), 0, "e4m3")
    ubar_q = mxq(ubar, 0, "e4m3")
    vbar_q = mxq(vbar, 0, "e4m3")
    return (au_q.T @ v_q) - (ubar_q.T @ vbar_q)

@@ -1,0 +1,452 @@
+from contextlib import ExitStack
+
+import concourse.mybir as mybir
+from concourse.masks import make_identity
+
+W, R, M, N = 4, 1024, 512, 1024
+FLOPS = 2 * W * R * M * N + 2 * R * M * N
+
+F32 = mybir.dt.float32
+BF16 = mybir.dt.bfloat16
+U32 = mybir.dt.uint32
+U8 = mybir.dt.uint8
+E4 = mybir.dt.float8_e4m3fn_x4
+E5 = mybir.dt.float8_e5m2_x4
+COPY = mybir.ActivationFunctionType.Copy
+MULT = mybir.AluOpType.mult
+
+P = 128
+PACK = 4
+QUAD = P // W
+ROWS = QUAD * PACK
+CHUNKS = R // ROWS
+GROUP = P * PACK // ROWS
+GROUPS = CHUNKS // GROUP
+HALF = 512
+MT = M // P
+NT = N // P
+NACC = 6
+
+
+def quad_view(dst, src):
+    return (
+        dst.rearrange("p (c i) t -> p c t i", i=4),
+        src.rearrange("p t (c i) -> p c t i", i=4),
+    )
+
+
+def tile_two_point_leonard_stress_s2_kernel(tc, u, v, a, out):
+    nc = tc.nc
+    u_rows = u.rearrange("w r i -> (w r) i")
+    v_rows = v.rearrange("w r j -> (w r) j")
+
+    with ExitStack() as ctx:
+        const = ctx.enter_context(tc.tile_pool(name="const", bufs=1))
+        keep = ctx.enter_context(tc.tile_pool(name="keep", bufs=1))
+        raw_u1 = ctx.enter_context(tc.tile_pool(name="raw_u1", bufs=2))
+        raw_u2 = ctx.enter_context(tc.tile_pool(name="raw_u2", bufs=3))
+        raw_v = ctx.enter_context(tc.tile_pool(name="raw_v", bufs=5))
+        grp_u = ctx.enter_context(tc.tile_pool(name="grp_u", bufs=3))
+        grp_v = ctx.enter_context(tc.tile_pool(name="grp_v", bufs=3))
+        sums = ctx.enter_context(tc.tile_pool(name="sums", bufs=2))
+        bars = ctx.enter_context(tc.tile_pool(name="bars", bufs=1))
+        outs = ctx.enter_context(tc.tile_pool(name="outs", bufs=8))
+        dps = ctx.enter_context(tc.psum_pool(name="dps", bufs=8 - NACC))
+        aps = ctx.enter_context(tc.psum_pool(name="aps", bufs=1))
+        ctx.enter_context(tc.manual_schedule())
+
+        u_codes = keep.tile([P, CHUNKS, M], U32, name="u_codes", align_bytes=256)
+        u_scales = keep.tile([P, CHUNKS, M], U8, name="u_scales", align_bytes=256)
+        v_codes = keep.tile([P, CHUNKS, N], U32, name="v_codes", align_bytes=256)
+        v_scales = keep.tile([P, CHUNKS, N], U8, name="v_scales", align_bytes=256)
+        ub_codes = keep.tile([P, GROUPS, M], U32, name="ub_codes", align_bytes=256)
+        ub_scales = keep.tile([P, GROUPS, M], U8, name="ub_scales", align_bytes=256)
+        vb_codes = keep.tile([P, GROUPS, N], U32, name="vb_codes", align_bytes=256)
+        vb_scales = keep.tile([P, GROUPS, N], U8, name="vb_scales", align_bytes=256)
+
+        u_raw = {}
+        v_raw = {}
+
+        def load_quadrants(dst, rows, chunk, count):
+            for w in (0, 2, 1, 3):
+                first = w * R + chunk * ROWS
+                part = rows[first : first + count * ROWS, :]
+                nc.sync.dma_start(
+                    out=dst[w * QUAD : (w + 1) * QUAD, :, :],
+                    in_=part.rearrange("(c q t) x -> q c (t x)", c=count, t=PACK),
+                )
+
+        def load_u(chunk, count):
+            pool = raw_u1 if count == 1 else raw_u2
+            t = pool.tile([P, count, PACK * M], BF16, name="u_raw%d" % count, align_bytes=64)
+            load_quadrants(t, u_rows, chunk, count)
+            for c in range(count):
+                u_raw[chunk + c] = t[:, c, :].rearrange("p (t i) -> p t i", t=PACK)
+
+        def load_v(chunk):
+            t = raw_v.tile([P, 1, PACK * N], BF16, name="v_raw", align_bytes=64)
+            load_quadrants(t, v_rows, chunk, 1)
+            v_raw[chunk] = t[:, 0, :].rearrange("p (t j) -> p t j", t=PACK)
+
+        def load_v_half(chunk, h):
+            if h == 0:
+                v_raw[chunk] = raw_v.tile([P, PACK, N], BF16, name="v_raw", align_bytes=64)
+            cols = slice(h * HALF, (h + 1) * HALF)
+            for w in (0, 2, 1, 3):
+                first = w * R + chunk * ROWS
+                nc.sync.dma_start(
+                    out=v_raw[chunk][w * QUAD : (w + 1) * QUAD, :, cols],
+                    in_=v_rows[first : first + ROWS, cols].rearrange("(q t) x -> q t x", t=PACK),
+                )
+
+        a_all = const.tile([P, W], BF16, name="a_all")
+        nc.sync.dma_start(out=a_all[:], in_=a.partition_broadcast(P))
+        load_v_half(0, 0)
+        load_u(0, 1)
+        load_v_half(0, 1)
+
+        ident = const.tile([P, P], F32, name="ident")
+        make_identity(nc, ident[:])
+        warm = const.tile([P, 1], F32, name="warm")
+        nc.vector.memset(warm[:], 0.0)
+        warm_out = const.tile([P, 1], F32, name="warm_out")
+        nc.scalar.activation(out=warm_out[:], in_=warm[:], func=COPY)
+        a_col = const.tile([P, 1], F32, name="a_col")
+        sel_v = const.tile([P, QUAD], BF16, name="sel_v")
+        sel_u = const.tile([P, QUAD], BF16, name="sel_u")
+        for w in range(W):
+            quad = slice(w * QUAD, (w + 1) * QUAD)
+            nc.vector.tensor_copy(out=a_col[quad, :], in_=a_all[quad, w : w + 1])
+        for w in range(W):
+            quad = slice(w * QUAD, (w + 1) * QUAD)
+            nc.vector.tensor_scalar(
+                out=sel_v[quad, :], in0=ident[quad, quad], scalar1=a_col[quad, :], scalar2=None, op0=MULT
+            )
+        nc.vector.tensor_scalar(out=sel_u[:], in0=sel_v[:], scalar1=-1.0, scalar2=None, op0=MULT)
+
+        u_grp = {}
+        v_grp = {}
+        sum_u = {}
+        sum_v = {}
+        bar_u = {}
+        bar_v = {}
+        acc = {}
+
+        def scale_u(c, part):
+            if part == 0:
+                u_grp[c] = grp_u.tile([P, M, PACK], BF16, name="u_grp", align_bytes=256)
+            cols = slice(part * M // 2, (part + 1) * M // 2)
+            dst, src = quad_view(u_grp[c][:, cols, :], u_raw[c][:, :, cols])
+            nc.scalar.activation(out=dst, in_=src, func=COPY, scale=a_col[:, 0:1])
+
+        def group_v(c, h):
+            g = grp_v.tile([P, HALF, PACK], BF16, name="v_grp", align_bytes=256)
+            dst, src = quad_view(g[:], v_raw[c][:, :, h * HALF : (h + 1) * HALF])
+            nc.vector.tensor_copy(out=dst, in_=src)
+            v_grp[c, h] = g
+
+        def quant_u(c):
+            nc.vector.quantize_mx(
+                out=u_codes[:, c, :].bitcast(E5),
+                scales=u_scales[:, c, :],
+                in_=u_grp[c][:].rearrange("p c t -> p (c t)"),
+            )
+
+        def quant_v(c, h):
+            cols = slice(h * HALF, (h + 1) * HALF)
+            nc.vector.quantize_mx(
+                out=v_codes[:, c, cols].bitcast(E4),
+                scales=v_scales[:, c, cols],
+                in_=v_grp[c, h][:].rearrange("p c t -> p (c t)"),
+            )
+
+        def sum_matmuls(bank, data, sel, blocks):
+            rhs = sel[:].rearrange("p (b y) -> p b y", b=4)
+            for blk in blocks:
+                for t in range(PACK):
+                    dst = bank[:, blk, t % 2, :].rearrange("j (b h y) -> j b h y", b=4, h=2)
+                    nc.tensor.matmul(
+                        out=dst[:, :, t // 2, :],
+                        lhsT=data[:, t, blk * P : (blk + 1) * P],
+                        rhs=rhs,
+                        start=True,
+                        stop=True,
+                    )
+
+        banks = {}
+
+        def sums_v(c, blocks=range(NT)):
+            if blocks[0] == 0:
+                banks["v", c] = dps.tile([P, NT, 2, 2 * QUAD], BF16, name="bank_sv", tag="d")
+            sum_matmuls(banks["v", c], v_raw[c], sel_v, blocks)
+
+        def sums_u(c):
+            banks["u", c] = dps.tile([P, MT, 2, 2 * QUAD], BF16, name="bank_su", tag="d")
+            sum_matmuls(banks["u", c], u_raw[c], sel_u, range(MT))
+
+        def keep_sums(kind, c):
+            group, slot = divmod(c, GROUP)
+            which, blocks = (sum_v, NT) if kind == "v" else (sum_u, MT)
+            if slot == 0:
+                which[group] = sums.tile([P, blocks, 2, 2 * P], BF16, name="sum_" + kind, align_bytes=64)
+            cols = slice(slot * 2 * QUAD, (slot + 1) * 2 * QUAD)
+            nc.scalar.copy(out=which[group][:, :, :, cols], in_=banks[kind, c][:])
+
+        def turn(kind, group, pair):
+            which = sum_v if kind == "v" else sum_u
+            bank = dps.tile([P, 2, 2 * P], F32, name="bank_t", tag="d")
+            for b in range(2):
+                for half in range(2):
+                    nc.tensor.transpose(
+                        bank[:, half, b * P : (b + 1) * P],
+                        which[group][:, 2 * pair + b, half, :].bitcast(F32),
+                        ident[:],
+                    )
+            banks[kind, group, pair] = bank
+
+        def keep_bar(kind, group, pair, engine="s"):
+            if pair == 0 and kind == "u":
+                bar_u[group] = bars.tile([P, M, PACK], BF16, name="bar_u", align_bytes=256)
+            if pair == 0 and kind == "v":
+                bar_v[group] = bars.tile([P, N, PACK], BF16, name="bar_v", align_bytes=256)
+            bar = (bar_v if kind == "v" else bar_u)[group]
+            words = bar[:, pair * 2 * P : (pair + 1) * 2 * P, :].rearrange("p c t -> p (c t)").bitcast(F32)
+            move = nc.scalar.copy if engine == "s" else nc.vector.tensor_copy
+            move(
+                out=words.rearrange("p (c h) -> p c h", h=2),
+                in_=banks[kind, group, pair][:].rearrange("p h c -> p c h"),
+            )
+
+        def quant_bar_u(group):
+            nc.vector.quantize_mx(
+                out=ub_codes[:, group, :].bitcast(E4),
+                scales=ub_scales[:, group, :],
+                in_=bar_u[group][:].rearrange("p c t -> p (c t)"),
+            )
+
+        def quant_bar_v(group, h):
+            cols = slice(h * HALF, (h + 1) * HALF)
+            nc.vector.quantize_mx(
+                out=vb_codes[:, group, cols].bitcast(E4),
+                scales=vb_scales[:, group, cols],
+                in_=bar_v[group][:, cols, :].rearrange("p c t -> p (c t)"),
+            )
+
+        TILES = [(mt, h) for h in range(2) for mt in range(MT)]
+        FIRST = TILES[:NACC]
+        SECOND = TILES[NACC:]
+
+        def mx(tiles, kind, k, start, stop):
+            if kind == "main":
+                lc, ls, lt, rc, rs = u_codes, u_scales, E5, v_codes, v_scales
+            else:
+                lc, ls, lt, rc, rs = ub_codes, ub_scales, E4, vb_codes, vb_scales
+            for mt, h in tiles:
+                ms = slice(mt * P, (mt + 1) * P)
+                ns = slice(h * HALF, (h + 1) * HALF)
+                nc.tensor.matmul_mx(
+                    out=acc[mt, h][:],
+                    lhsT=lc[:, k, ms].bitcast(lt),
+                    lhsT_scale=ls[:, k, ms],
+                    rhs=rc[:, k, ns].bitcast(E4),
+                    rhs_scale=rs[:, k, ns],
+                    start=start,
+                    stop=stop,
+                )
+
+        def store(tiles, engines):
+            for n, (mt, h) in enumerate(tiles):
+                res = outs.tile([P, HALF], F32, name="res")
+                if engines[n % len(engines)] == "v":
+                    nc.vector.tensor_copy(out=res[:], in_=acc[mt, h][:])
+                else:
+                    nc.scalar.copy(out=res[:], in_=acc[mt, h][:])
+                nc.sync.dma_start(
+                    out=out[mt * P : (mt + 1) * P, h * HALF : (h + 1) * HALF], in_=res[:]
+                )
+
+        for n, key in enumerate(FIRST):
+            acc[key] = aps.tile([P, HALF], F32, name="acc%d" % n)
+
+        def loads(which):
+            kind, c, count = which
+            if kind == "u":
+                load_u(c, count)
+            else:
+                load_v(c)
+
+        def au(i):
+            scale_u(i, 0)
+            scale_u(i, 1)
+
+        jobs = []
+
+        def add(tiles, kind, k):
+            jobs.extend((tile, kind, k) for tile in tiles)
+
+        opened = set()
+
+        taken = [0]
+
+        def fill(count):
+            for tile, kind, k in jobs[taken[0] : taken[0] + count]:
+                closing = kind == "main" and k == CHUNKS - 1
+                mx([tile], kind, k, tile not in opened, closing)
+                opened.add(tile)
+            taken[0] = min(taken[0] + count, len(jobs))
+
+        for which in (("v", 1, 1), ("u", 1, 1), ("v", 2, 1), ("u", 2, 2), ("v", 3, 1), ("v", 4, 1), ("u", 4, 2)):
+            loads(which)
+        sums_v(0, range(0, 4))
+        scale_u(0, 0)
+        sums_u(0)
+        sums_v(0, range(4, 8))
+        scale_u(0, 1)
+        keep_sums("v", 0)
+        keep_sums("u", 0)
+        group_v(0, 0)
+        group_v(0, 1)
+        quant_v(0, 0)
+        quant_u(0)
+        quant_v(0, 1)
+        add(FIRST, "main", 0)
+        loads(("v", 5, 1))
+        loads(("u", 6, 2))
+        sums_v(1)
+        keep_sums("v", 1)
+        fill(4)
+        scale_u(1, 0)
+        sums_u(1)
+        scale_u(1, 1)
+        keep_sums("u", 1)
+        fill(2)
+        group_v(1, 0)
+        group_v(1, 1)
+        quant_v(1, 0)
+        quant_u(1)
+        sums_v(2)
+        keep_sums("v", 2)
+        sums_u(2)
+        scale_u(2, 0)
+        scale_u(2, 1)
+        keep_sums("u", 2)
+        group_v(2, 0)
+        quant_v(1, 1)
+        group_v(2, 1)
+        quant_v(2, 0)
+        quant_u(2)
+        add(FIRST, "main", 1)
+        fill(6)
+        loads(("v", 6, 1))
+        sums_v(3)
+        scale_u(3, 0)
+        scale_u(3, 1)
+        keep_sums("v", 3)
+        sums_u(3)
+        keep_sums("u", 3)
+        group_v(3, 0)
+        quant_v(2, 1)
+        group_v(3, 1)
+        quant_v(3, 0)
+        quant_u(3)
+        add(FIRST, "main", 2)
+        loads(("v", 7, 1))
+        sums_v(4)
+        turn("u", 0, 0)
+        keep_sums("v", 4)
+        keep_bar("u", 0, 0)
+        fill(2)
+        sums_u(4)
+        fill(2)
+        turn("u", 0, 1)
+        keep_sums("u", 4)
+        keep_bar("u", 0, 1)
+        fill(2)
+        scale_u(4, 0)
+        scale_u(4, 1)
+        group_v(4, 0)
+        quant_v(3, 1)
+        group_v(4, 1)
+        quant_v(4, 0)
+        quant_u(4)
+        quant_bar_u(0)
+        add(FIRST, "main", 3)
+        turn("v", 0, 0)
+        keep_bar("v", 0, 0)
+        sums_v(5)
+        keep_sums("v", 5)
+        fill(2)
+        turn("v", 0, 1)
+        keep_bar("v", 0, 1)
+        sums_u(5)
+        keep_sums("u", 5)
+        fill(4)
+        au(5)
+        group_v(5, 0)
+        quant_v(4, 1)
+        group_v(5, 1)
+        quant_v(5, 0)
+        quant_bar_v(0, 0)
+        quant_u(5)
+        add(FIRST, "main", 4)
+        turn("v", 0, 2)
+        keep_bar("v", 0, 2)
+        turn("v", 0, 3)
+        keep_bar("v", 0, 3)
+        sums_v(6)
+        keep_sums("v", 6)
+        sums_u(6)
+        keep_sums("u", 6)
+        fill(3)
+        sums_v(7)
+        keep_sums("v", 7)
+        sums_u(7)
+        keep_sums("u", 7)
+        fill(3)
+        quant_bar_v(0, 1)
+        add(FIRST, "bar", 0)
+        turn("u", 1, 0)
+        turn("u", 1, 1)
+        keep_bar("u", 1, 0)
+        keep_bar("u", 1, 1)
+        fill(3)
+        turn("v", 1, 0)
+        turn("v", 1, 1)
+        keep_bar("v", 1, 0)
+        keep_bar("v", 1, 1)
+        au(6)
+        fill(3)
+        turn("v", 1, 2)
+        turn("v", 1, 3)
+        keep_bar("v", 1, 2)
+        keep_bar("v", 1, 3)
+        group_v(6, 0)
+        quant_v(5, 1)
+        add(FIRST, "main", 5)
+        group_v(6, 1)
+        quant_v(6, 0)
+        quant_u(6)
+        fill(6)
+        for key in SECOND:
+            acc[key] = dps.tile([P, HALF], F32, name="acc_late", tag="d")
+        for c in range(6):
+            add(SECOND, "main", c)
+        add(SECOND, "bar", 0)
+        fill(len(jobs))
+        au(7)
+        group_v(7, 0)
+        quant_v(6, 1)
+        add(TILES, "main", 6)
+        fill(len(jobs))
+        quant_bar_u(1)
+        group_v(7, 1)
+        quant_bar_v(1, 0)
+        quant_bar_v(1, 1)
+        add(TILES, "bar", 1)
+        fill(len(jobs))
+        quant_v(7, 0)
+        quant_u(7)
+        quant_v(7, 1)
+        add(TILES, "main", 7)
+        fill(len(jobs))
+        store(TILES, "sv")

@@ -25,14 +25,8 @@ GROUPS = CHUNKS // GROUP
 HALF = 512
 MT = M // P
 NT = N // P
-NACC = 6
-
-
-def quad_view(dst, src):
-    return (
-        dst.rearrange("p (c i) t -> p c t i", i=4),
-        src.rearrange("p t (c i) -> p c t i", i=4),
-    )
+PASSES = CHUNKS + GROUPS
+LATE = [(2, 1), (3, 1)]
 
 
 def tile_two_point_leonard_stress_s2_kernel(tc, u, v, a, out):
@@ -43,15 +37,14 @@ def tile_two_point_leonard_stress_s2_kernel(tc, u, v, a, out):
     with ExitStack() as ctx:
         const = ctx.enter_context(tc.tile_pool(name="const", bufs=1))
         keep = ctx.enter_context(tc.tile_pool(name="keep", bufs=1))
-        raw_u1 = ctx.enter_context(tc.tile_pool(name="raw_u1", bufs=2))
-        raw_u2 = ctx.enter_context(tc.tile_pool(name="raw_u2", bufs=3))
-        raw_v = ctx.enter_context(tc.tile_pool(name="raw_v", bufs=5))
+        raw_u = ctx.enter_context(tc.tile_pool(name="raw_u", bufs=1))
+        raw_v = ctx.enter_context(tc.tile_pool(name="raw_v", bufs=3))
         grp_u = ctx.enter_context(tc.tile_pool(name="grp_u", bufs=3))
         grp_v = ctx.enter_context(tc.tile_pool(name="grp_v", bufs=3))
         sums = ctx.enter_context(tc.tile_pool(name="sums", bufs=2))
         bars = ctx.enter_context(tc.tile_pool(name="bars", bufs=1))
-        outs = ctx.enter_context(tc.tile_pool(name="outs", bufs=8))
-        dps = ctx.enter_context(tc.psum_pool(name="dps", bufs=8 - NACC))
+        outs = ctx.enter_context(tc.tile_pool(name="outs", bufs=4))
+        dps = ctx.enter_context(tc.psum_pool(name="dps", bufs=2))
         aps = ctx.enter_context(tc.psum_pool(name="aps", bufs=1))
         ctx.enter_context(tc.manual_schedule())
 
@@ -64,65 +57,57 @@ def tile_two_point_leonard_stress_s2_kernel(tc, u, v, a, out):
         vb_codes = keep.tile([P, GROUPS, N], U32, name="vb_codes", align_bytes=256)
         vb_scales = keep.tile([P, GROUPS, N], U8, name="vb_scales", align_bytes=256)
 
-        u_raw = {}
-        v_raw = {}
+        u_all = raw_u.tile([P, CHUNKS, PACK, M], BF16, name="u_all", align_bytes=256)
+        v_pair = {}
 
-        def load_quadrants(dst, rows, chunk, count):
-            for w in (0, 2, 1, 3):
+        def ld(kind, queue, chunk, count, c0=0, c1=N):
+            if kind == "u":
+                dst, src, cols, at = u_all, u_rows, slice(0, M), chunk
+            else:
+                pair = chunk // 2
+                if pair not in v_pair:
+                    v_pair[pair] = raw_v.tile([P, 2, PACK, N], BF16, name="v_pair", align_bytes=256)
+                dst, src, cols, at = v_pair[pair], v_rows, slice(c0, c1), chunk % 2
+            for w in (0, 1) if queue == "sp" else (2, 3):
                 first = w * R + chunk * ROWS
-                part = rows[first : first + count * ROWS, :]
-                nc.sync.dma_start(
-                    out=dst[w * QUAD : (w + 1) * QUAD, :, :],
-                    in_=part.rearrange("(c q t) x -> q c (t x)", c=count, t=PACK),
-                )
+                eng = nc.sync if queue == "sp" else nc.scalar
+                part = src[first : first + count * ROWS, cols]
+                to = dst[w * QUAD : (w + 1) * QUAD, at : at + count, :, cols]
+                if cols.stop - cols.start == src.shape[1]:
+                    eng.dma_start(
+                        out=to.rearrange("q c t x -> q c (t x)"),
+                        in_=part.rearrange("(c q t) x -> q c (t x)", c=count, t=PACK),
+                    )
+                else:
+                    eng.dma_start(
+                        out=to.rearrange("q c t x -> q (c t) x"),
+                        in_=part.rearrange("(q t) x -> q t x", t=PACK),
+                    )
 
-        def load_u(chunk, count):
-            pool = raw_u1 if count == 1 else raw_u2
-            t = pool.tile([P, count, PACK * M], BF16, name="u_raw%d" % count, align_bytes=64)
-            load_quadrants(t, u_rows, chunk, count)
-            for c in range(count):
-                u_raw[chunk + c] = t[:, c, :].rearrange("p (t i) -> p t i", t=PACK)
+        def u_raw(c):
+            return u_all[:, c, :, :]
 
-        def load_v(chunk):
-            t = raw_v.tile([P, 1, PACK * N], BF16, name="v_raw", align_bytes=64)
-            load_quadrants(t, v_rows, chunk, 1)
-            v_raw[chunk] = t[:, 0, :].rearrange("p (t j) -> p t j", t=PACK)
-
-        def load_v_half(chunk, h):
-            if h == 0:
-                v_raw[chunk] = raw_v.tile([P, PACK, N], BF16, name="v_raw", align_bytes=64)
-            cols = slice(h * HALF, (h + 1) * HALF)
-            for w in (0, 2, 1, 3):
-                first = w * R + chunk * ROWS
-                nc.sync.dma_start(
-                    out=v_raw[chunk][w * QUAD : (w + 1) * QUAD, :, cols],
-                    in_=v_rows[first : first + ROWS, cols].rearrange("(q t) x -> q t x", t=PACK),
-                )
+        def v_raw(c):
+            return v_pair[c // 2][:, c % 2, :, :]
 
         a_all = const.tile([P, W], BF16, name="a_all")
-        nc.sync.dma_start(out=a_all[:], in_=a.partition_broadcast(P))
-        load_v_half(0, 0)
-        load_u(0, 1)
-        load_v_half(0, 1)
-
         ident = const.tile([P, P], F32, name="ident")
-        make_identity(nc, ident[:])
         warm = const.tile([P, 1], F32, name="warm")
-        nc.vector.memset(warm[:], 0.0)
         warm_out = const.tile([P, 1], F32, name="warm_out")
-        nc.scalar.activation(out=warm_out[:], in_=warm[:], func=COPY)
         a_col = const.tile([P, 1], F32, name="a_col")
         sel_v = const.tile([P, QUAD], BF16, name="sel_v")
         sel_u = const.tile([P, QUAD], BF16, name="sel_u")
-        for w in range(W):
-            quad = slice(w * QUAD, (w + 1) * QUAD)
-            nc.vector.tensor_copy(out=a_col[quad, :], in_=a_all[quad, w : w + 1])
-        for w in range(W):
-            quad = slice(w * QUAD, (w + 1) * QUAD)
-            nc.vector.tensor_scalar(
-                out=sel_v[quad, :], in0=ident[quad, quad], scalar1=a_col[quad, :], scalar2=None, op0=MULT
-            )
-        nc.vector.tensor_scalar(out=sel_u[:], in0=sel_v[:], scalar1=-1.0, scalar2=None, op0=MULT)
+
+        def constants():
+            for w in range(W):
+                quad = slice(w * QUAD, (w + 1) * QUAD)
+                nc.vector.tensor_copy(out=a_col[quad, :], in_=a_all[quad, w : w + 1])
+            for w in range(W):
+                quad = slice(w * QUAD, (w + 1) * QUAD)
+                nc.vector.tensor_scalar(
+                    out=sel_v[quad, :], in0=ident[quad, quad], scalar1=a_col[quad, :], scalar2=None, op0=MULT
+                )
+            nc.vector.tensor_scalar(out=sel_u[:], in0=sel_v[:], scalar1=-1.0, scalar2=None, op0=MULT)
 
         u_grp = {}
         v_grp = {}
@@ -130,29 +115,36 @@ def tile_two_point_leonard_stress_s2_kernel(tc, u, v, a, out):
         sum_v = {}
         bar_u = {}
         bar_v = {}
+        banks = {}
         acc = {}
 
-        def scale_u(c, part):
+        def spread(dst, src):
+            return (
+                dst.rearrange("p (c i) t -> p c t i", i=4),
+                src.rearrange("p t (c i) -> p c t i", i=4),
+            )
+
+        def au(c, part):
             if part == 0:
                 u_grp[c] = grp_u.tile([P, M, PACK], BF16, name="u_grp", align_bytes=256)
             cols = slice(part * M // 2, (part + 1) * M // 2)
-            dst, src = quad_view(u_grp[c][:, cols, :], u_raw[c][:, :, cols])
+            dst, src = spread(u_grp[c][:, cols, :], u_raw(c)[:, :, cols])
             nc.scalar.activation(out=dst, in_=src, func=COPY, scale=a_col[:, 0:1])
 
-        def group_v(c, h):
+        def gv(c, h):
             g = grp_v.tile([P, HALF, PACK], BF16, name="v_grp", align_bytes=256)
-            dst, src = quad_view(g[:], v_raw[c][:, :, h * HALF : (h + 1) * HALF])
+            dst, src = spread(g[:], v_raw(c)[:, :, h * HALF : (h + 1) * HALF])
             nc.vector.tensor_copy(out=dst, in_=src)
             v_grp[c, h] = g
 
-        def quant_u(c):
+        def qu(c):
             nc.vector.quantize_mx(
                 out=u_codes[:, c, :].bitcast(E5),
                 scales=u_scales[:, c, :],
                 in_=u_grp[c][:].rearrange("p c t -> p (c t)"),
             )
 
-        def quant_v(c, h):
+        def qv(c, h):
             cols = slice(h * HALF, (h + 1) * HALF)
             nc.vector.quantize_mx(
                 out=v_codes[:, c, cols].bitcast(E4),
@@ -173,18 +165,17 @@ def tile_two_point_leonard_stress_s2_kernel(tc, u, v, a, out):
                         stop=True,
                     )
 
-        banks = {}
-
-        def sums_v(c, blocks=range(NT)):
-            if blocks[0] == 0:
+        def sv(c, part=None):
+            if part != 1:
                 banks["v", c] = dps.tile([P, NT, 2, 2 * QUAD], BF16, name="bank_sv", tag="d")
-            sum_matmuls(banks["v", c], v_raw[c], sel_v, blocks)
+            blocks = {None: range(NT), 0: range(NT // 2), 1: range(NT // 2, NT)}[part]
+            sum_matmuls(banks["v", c], v_raw(c), sel_v, blocks)
 
-        def sums_u(c):
+        def su(c):
             banks["u", c] = dps.tile([P, MT, 2, 2 * QUAD], BF16, name="bank_su", tag="d")
-            sum_matmuls(banks["u", c], u_raw[c], sel_u, range(MT))
+            sum_matmuls(banks["u", c], u_raw(c), sel_u, range(MT))
 
-        def keep_sums(kind, c):
+        def ks(kind, c):
             group, slot = divmod(c, GROUP)
             which, blocks = (sum_v, NT) if kind == "v" else (sum_u, MT)
             if slot == 0:
@@ -204,7 +195,7 @@ def tile_two_point_leonard_stress_s2_kernel(tc, u, v, a, out):
                     )
             banks[kind, group, pair] = bank
 
-        def keep_bar(kind, group, pair, engine="s"):
+        def kb(kind, group, pair, engine="s"):
             if pair == 0 and kind == "u":
                 bar_u[group] = bars.tile([P, M, PACK], BF16, name="bar_u", align_bytes=256)
             if pair == 0 and kind == "v":
@@ -217,14 +208,14 @@ def tile_two_point_leonard_stress_s2_kernel(tc, u, v, a, out):
                 in_=banks[kind, group, pair][:].rearrange("p h c -> p c h"),
             )
 
-        def quant_bar_u(group):
+        def qbu(group):
             nc.vector.quantize_mx(
                 out=ub_codes[:, group, :].bitcast(E4),
                 scales=ub_scales[:, group, :],
                 in_=bar_u[group][:].rearrange("p c t -> p (c t)"),
             )
 
-        def quant_bar_v(group, h):
+        def qbv(group, h):
             cols = slice(h * HALF, (h + 1) * HALF)
             nc.vector.quantize_mx(
                 out=vb_codes[:, group, cols].bitcast(E4),
@@ -232,221 +223,285 @@ def tile_two_point_leonard_stress_s2_kernel(tc, u, v, a, out):
                 in_=bar_v[group][:, cols, :].rearrange("p c t -> p (c t)"),
             )
 
-        TILES = [(mt, h) for h in range(2) for mt in range(MT)]
-        FIRST = TILES[:NACC]
-        SECOND = TILES[NACC:]
+        done = {}
 
-        def mx(tiles, kind, k, start, stop):
+        def mx(mt, h, kind, k):
             if kind == "main":
                 lc, ls, lt, rc, rs = u_codes, u_scales, E5, v_codes, v_scales
             else:
                 lc, ls, lt, rc, rs = ub_codes, ub_scales, E4, vb_codes, vb_scales
-            for mt, h in tiles:
-                ms = slice(mt * P, (mt + 1) * P)
-                ns = slice(h * HALF, (h + 1) * HALF)
-                nc.tensor.matmul_mx(
-                    out=acc[mt, h][:],
-                    lhsT=lc[:, k, ms].bitcast(lt),
-                    lhsT_scale=ls[:, k, ms],
-                    rhs=rc[:, k, ns].bitcast(E4),
-                    rhs_scale=rs[:, k, ns],
-                    start=start,
-                    stop=stop,
-                )
-
-        def store(tiles, engines):
-            for n, (mt, h) in enumerate(tiles):
-                res = outs.tile([P, HALF], F32, name="res")
-                if engines[n % len(engines)] == "v":
-                    nc.vector.tensor_copy(out=res[:], in_=acc[mt, h][:])
+            key = (mt, h)
+            if key not in acc:
+                if key in LATE:
+                    acc[key] = dps.tile([P, HALF], F32, name="acc_late", tag="d")
                 else:
-                    nc.scalar.copy(out=res[:], in_=acc[mt, h][:])
-                nc.sync.dma_start(
-                    out=out[mt * P : (mt + 1) * P, h * HALF : (h + 1) * HALF], in_=res[:]
-                )
+                    acc[key] = aps.tile([P, HALF], F32, name="acc%d" % (mt + MT * h))
+            ms = slice(mt * P, (mt + 1) * P)
+            ns = slice(h * HALF, (h + 1) * HALF)
+            done[key] = done.get(key, 0) + 1
+            nc.tensor.matmul_mx(
+                out=acc[key][:],
+                lhsT=lc[:, k, ms].bitcast(lt),
+                lhsT_scale=ls[:, k, ms],
+                rhs=rc[:, k, ns].bitcast(E4),
+                rhs_scale=rs[:, k, ns],
+                start=done[key] == 1,
+                stop=done[key] == PASSES,
+            )
 
-        for n, key in enumerate(FIRST):
-            acc[key] = aps.tile([P, HALF], F32, name="acc%d" % n)
+        res = {}
 
-        def loads(which):
-            kind, c, count = which
-            if kind == "u":
-                load_u(c, count)
+        def oc(mt, h, engine):
+            res[mt, h] = outs.tile([P, HALF], F32, name="res")
+            if engine == "v":
+                nc.vector.tensor_copy(out=res[mt, h][:], in_=acc[mt, h][:])
             else:
-                load_v(c)
+                nc.scalar.copy(out=res[mt, h][:], in_=acc[mt, h][:])
 
-        def au(i):
-            scale_u(i, 0)
-            scale_u(i, 1)
+        def st(mt, h):
+            nc.sync.dma_start(
+                out=out[mt * P : (mt + 1) * P, h * HALF : (h + 1) * HALF], in_=res[mt, h][:]
+            )
 
-        jobs = []
-
-        def add(tiles, kind, k):
-            jobs.extend((tile, kind, k) for tile in tiles)
-
-        opened = set()
-
-        taken = [0]
-
-        def fill(count):
-            for tile, kind, k in jobs[taken[0] : taken[0] + count]:
-                closing = kind == "main" and k == CHUNKS - 1
-                mx([tile], kind, k, tile not in opened, closing)
-                opened.add(tile)
-            taken[0] = min(taken[0] + count, len(jobs))
-
-        for which in (("v", 1, 1), ("u", 1, 1), ("v", 2, 1), ("u", 2, 2), ("v", 3, 1), ("v", 4, 1), ("u", 4, 2)):
-            loads(which)
-        sums_v(0, range(0, 4))
-        scale_u(0, 0)
-        sums_u(0)
-        sums_v(0, range(4, 8))
-        scale_u(0, 1)
-        keep_sums("v", 0)
-        keep_sums("u", 0)
-        group_v(0, 0)
-        group_v(0, 1)
-        quant_v(0, 0)
-        quant_u(0)
-        quant_v(0, 1)
-        add(FIRST, "main", 0)
-        loads(("v", 5, 1))
-        loads(("u", 6, 2))
-        sums_v(1)
-        keep_sums("v", 1)
-        fill(4)
-        scale_u(1, 0)
-        sums_u(1)
-        scale_u(1, 1)
-        keep_sums("u", 1)
-        fill(2)
-        group_v(1, 0)
-        group_v(1, 1)
-        quant_v(1, 0)
-        quant_u(1)
-        sums_v(2)
-        keep_sums("v", 2)
-        sums_u(2)
-        scale_u(2, 0)
-        scale_u(2, 1)
-        keep_sums("u", 2)
-        group_v(2, 0)
-        quant_v(1, 1)
-        group_v(2, 1)
-        quant_v(2, 0)
-        quant_u(2)
-        add(FIRST, "main", 1)
-        fill(6)
-        loads(("v", 6, 1))
-        sums_v(3)
-        scale_u(3, 0)
-        scale_u(3, 1)
-        keep_sums("v", 3)
-        sums_u(3)
-        keep_sums("u", 3)
-        group_v(3, 0)
-        quant_v(2, 1)
-        group_v(3, 1)
-        quant_v(3, 0)
-        quant_u(3)
-        add(FIRST, "main", 2)
-        loads(("v", 7, 1))
-        sums_v(4)
+        nc.sync.dma_start(out=a_all[:], in_=a.partition_broadcast(P))
+        ld("v", "act", 0, 1, 0, 512)
+        make_identity(nc, ident[:])
+        nc.vector.memset(warm[:], 0.0)
+        ld("v", "sp", 0, 1, 0, 512)
+        ld("u", "act", 0, 1)
+        ld("u", "sp", 0, 1)
+        ld("v", "act", 0, 1, 512, 1024)
+        constants()
+        ld("v", "sp", 0, 1, 512, 1024)
+        ld("v", "act", 1, 1)
+        sv(0, 0)
+        gv(0, 0)
+        ld("v", "sp", 1, 1)
+        nc.scalar.activation(out=warm_out[:], in_=warm[:], func=COPY)
+        ld("u", "act", 1, 1)
+        su(0)
+        ld("u", "sp", 1, 1)
+        qv(0, 0)
+        au(0, 0)
+        sv(0, 1)
+        gv(0, 1)
+        ld("v", "sp", 2, 1)
+        au(0, 1)
+        ld("u", "sp", 2, 2)
+        qv(0, 1)
+        ks("v", 0)
+        qu(0)
+        ld("v", "act", 2, 1)
+        sv(1)
+        ld("v", "sp", 3, 1)
+        gv(1, 1)
+        ks("u", 0)
+        mx(3, 0, "main", 0)
+        ld("u", "act", 2, 2)
+        mx(1, 1, "main", 0)
+        ld("v", "sp", 4, 2)
+        mx(1, 0, "main", 0)
+        gv(1, 0)
+        mx(0, 1, "main", 0)
+        su(1)
+        mx(2, 0, "main", 0)
+        mx(0, 0, "main", 0)
+        qv(1, 1)
+        au(1, 0)
+        qv(1, 0)
+        ld("v", "act", 3, 1)
+        gv(2, 1)
+        ld("u", "sp", 4, 4)
+        ks("u", 1)
+        gv(2, 0)
+        ks("v", 1)
+        au(1, 1)
+        sv(2)
+        ld("v", "sp", 6, 2)
+        qv(2, 1)
+        su(2)
+        qv(2, 0)
+        au(2, 0)
+        qu(1)
+        ks("u", 2)
+        mx(1, 1, "main", 1)
+        ld("v", "act", 4, 2)
+        mx(0, 0, "main", 1)
+        gv(3, 0)
+        au(3, 0)
+        mx(0, 1, "main", 1)
+        mx(3, 0, "main", 1)
+        mx(1, 0, "main", 1)
+        su(3)
+        ks("v", 2)
+        gv(3, 1)
+        mx(2, 0, "main", 1)
+        au(3, 1)
+        sv(3)
+        qv(3, 0)
+        ks("u", 3)
+        ks("v", 3)
+        qu(3)
+        ld("u", "act", 4, 4)
+        qv(3, 1)
         turn("u", 0, 0)
-        keep_sums("v", 4)
-        keep_bar("u", 0, 0)
-        fill(2)
-        sums_u(4)
-        fill(2)
+        au(2, 1)
+        mx(0, 0, "main", 3)
+        mx(0, 1, "main", 3)
+        mx(1, 0, "main", 3)
+        mx(1, 1, "main", 3)
+        kb("u", 0, 0)
+        mx(3, 0, "main", 3)
+        qu(2)
+        mx(2, 0, "main", 3)
+        ld("v", "act", 6, 2)
         turn("u", 0, 1)
-        keep_sums("u", 4)
-        keep_bar("u", 0, 1)
-        fill(2)
-        scale_u(4, 0)
-        scale_u(4, 1)
-        group_v(4, 0)
-        quant_v(3, 1)
-        group_v(4, 1)
-        quant_v(4, 0)
-        quant_u(4)
-        quant_bar_u(0)
-        add(FIRST, "main", 3)
+        mx(3, 0, "main", 2)
+        gv(5, 0)
+        kb("u", 0, 1)
+        sv(4)
         turn("v", 0, 0)
-        keep_bar("v", 0, 0)
-        sums_v(5)
-        keep_sums("v", 5)
-        fill(2)
+        qbu(0)
+        ks("v", 4)
+        mx(0, 0, "main", 2)
+        mx(0, 1, "main", 2)
+        qv(5, 0)
+        kb("v", 0, 0)
+        mx(1, 0, "main", 2)
+        mx(1, 1, "main", 2)
+        gv(4, 0)
+        mx(2, 0, "main", 2)
         turn("v", 0, 1)
-        keep_bar("v", 0, 1)
-        sums_u(5)
-        keep_sums("u", 5)
-        fill(4)
-        au(5)
-        group_v(5, 0)
-        quant_v(4, 1)
-        group_v(5, 1)
-        quant_v(5, 0)
-        quant_bar_v(0, 0)
-        quant_u(5)
-        add(FIRST, "main", 4)
+        kb("v", 0, 1)
+        gv(4, 1)
         turn("v", 0, 2)
-        keep_bar("v", 0, 2)
+        su(4)
+        au(4, 0)
+        qv(4, 0)
+        qv(4, 1)
+        ks("u", 4)
+        qbv(0, 0)
+        kb("v", 0, 2)
+        sv(5)
+        gv(5, 1)
+        au(4, 1)
         turn("v", 0, 3)
-        keep_bar("v", 0, 3)
-        sums_v(6)
-        keep_sums("v", 6)
-        sums_u(6)
-        keep_sums("u", 6)
-        fill(3)
-        sums_v(7)
-        keep_sums("v", 7)
-        sums_u(7)
-        keep_sums("u", 7)
-        fill(3)
-        quant_bar_v(0, 1)
-        add(FIRST, "bar", 0)
+        mx(1, 0, "bar", 0)
+        mx(3, 0, "bar", 0)
+        ks("v", 5)
+        qu(4)
+        mx(0, 0, "bar", 0)
+        mx(2, 0, "bar", 0)
+        au(5, 0)
+        qv(5, 1)
+        su(5)
+        mx(1, 0, "main", 4)
+        mx(0, 1, "main", 4)
+        gv(6, 1)
+        ks("u", 5)
+        mx(0, 0, "main", 4)
+        kb("v", 0, 3)
+        mx(1, 1, "main", 4)
+        mx(3, 0, "main", 4)
+        au(6, 0)
+        mx(2, 0, "main", 4)
+        qbv(0, 1)
+        sv(6)
+        gv(7, 0)
+        au(5, 1)
+        mx(0, 1, "bar", 0)
+        mx(1, 1, "bar", 0)
+        sv(7)
+        qv(6, 1)
+        ks("v", 6)
+        qu(5)
+        au(6, 1)
+        su(6)
+        gv(6, 0)
+        mx(2, 0, "main", 5)
+        mx(0, 1, "main", 5)
+        ks("u", 6)
+        mx(3, 0, "main", 5)
+        ks("v", 7)
+        mx(1, 1, "main", 5)
+        qu(6)
+        su(7)
+        au(7, 0)
+        mx(0, 0, "main", 5)
+        qv(6, 0)
+        mx(0, 1, "main", 6)
+        mx(1, 1, "main", 6)
+        qv(7, 0)
+        ks("u", 7)
+        mx(1, 0, "main", 6)
+        au(7, 1)
+        mx(3, 0, "main", 6)
+        gv(7, 1)
+        mx(0, 0, "main", 6)
         turn("u", 1, 0)
         turn("u", 1, 1)
-        keep_bar("u", 1, 0)
-        keep_bar("u", 1, 1)
-        fill(3)
+        kb("u", 1, 0)
+        mx(2, 0, "main", 6)
+        qu(7)
+        mx(1, 0, "main", 5)
+        kb("u", 1, 1)
         turn("v", 1, 0)
-        turn("v", 1, 1)
-        keep_bar("v", 1, 0)
-        keep_bar("v", 1, 1)
-        au(6)
-        fill(3)
+        qv(7, 1)
+        mx(2, 0, "main", 7)
+        qbu(1)
+        kb("v", 1, 0)
+        mx(1, 0, "main", 7)
+        mx(3, 0, "main", 7)
+        mx(0, 1, "main", 7)
         turn("v", 1, 2)
+        turn("v", 1, 1)
+        kb("v", 1, 2)
+        mx(0, 0, "main", 7)
+        mx(1, 1, "main", 7)
+        kb("v", 1, 1)
+        mx(2, 1, "main", 1)
+        mx(2, 1, "bar", 0)
+        mx(2, 1, "main", 7)
+        qbv(1, 0)
+        mx(2, 1, "main", 3)
+        mx(2, 1, "main", 6)
+        mx(0, 0, "bar", 1)
+        mx(3, 0, "bar", 1)
+        mx(2, 0, "bar", 1)
+        oc(0, 0, "s")
         turn("v", 1, 3)
-        keep_bar("v", 1, 2)
-        keep_bar("v", 1, 3)
-        group_v(6, 0)
-        quant_v(5, 1)
-        add(FIRST, "main", 5)
-        group_v(6, 1)
-        quant_v(6, 0)
-        quant_u(6)
-        fill(6)
-        for key in SECOND:
-            acc[key] = dps.tile([P, HALF], F32, name="acc_late", tag="d")
-        for c in range(6):
-            add(SECOND, "main", c)
-        add(SECOND, "bar", 0)
-        fill(len(jobs))
-        au(7)
-        group_v(7, 0)
-        quant_v(6, 1)
-        add(TILES, "main", 6)
-        fill(len(jobs))
-        quant_bar_u(1)
-        group_v(7, 1)
-        quant_bar_v(1, 0)
-        quant_bar_v(1, 1)
-        add(TILES, "bar", 1)
-        fill(len(jobs))
-        quant_v(7, 0)
-        quant_u(7)
-        quant_v(7, 1)
-        add(TILES, "main", 7)
-        fill(len(jobs))
-        store(TILES, "sv")
+        oc(3, 0, "v")
+        oc(2, 0, "s")
+        mx(2, 1, "main", 5)
+        st(0, 0)
+        st(3, 0)
+        mx(1, 0, "bar", 1)
+        kb("v", 1, 3)
+        mx(2, 1, "main", 0)
+        st(2, 0)
+        mx(2, 1, "main", 2)
+        oc(1, 0, "v")
+        mx(2, 1, "main", 4)
+        mx(3, 1, "main", 5)
+        qbv(1, 1)
+        st(1, 0)
+        mx(3, 1, "main", 4)
+        mx(3, 1, "main", 7)
+        mx(0, 1, "bar", 1)
+        mx(3, 1, "bar", 1)
+        mx(2, 1, "bar", 1)
+        oc(0, 1, "s")
+        mx(3, 1, "main", 6)
+        mx(3, 1, "main", 0)
+        st(0, 1)
+        mx(1, 1, "bar", 1)
+        oc(2, 1, "s")
+        mx(3, 1, "bar", 0)
+        mx(3, 1, "main", 2)
+        oc(1, 1, "v")
+        st(2, 1)
+        mx(3, 1, "main", 1)
+        mx(3, 1, "main", 3)
+        st(1, 1)
+        oc(3, 1, "v")
+        st(3, 1)

@@ -14,18 +14,20 @@ E4 = mybir.dt.float8_e4m3fn_x4
 E5 = mybir.dt.float8_e5m2_x4
 COPY = mybir.ActivationFunctionType.Copy
 MULT = mybir.AluOpType.mult
+ADD = mybir.AluOpType.add
 
 P = 128
 PACK = 4
+ROWS = P * PACK
+GROUPS = R // ROWS
+CHUNKS = W * GROUPS
 QUAD = P // W
-ROWS = QUAD * PACK
-CHUNKS = R // ROWS
-GROUP = P * PACK // ROWS
-GROUPS = CHUNKS // GROUP
+RUN = W * R // P
 HALF = 512
 MT = M // P
-NT = N // P
+BLK = HALF // P
 PASSES = CHUNKS + GROUPS
+V_COLS = 512
 LATE = [(2, 1), (3, 1)]
 
 
@@ -37,13 +39,11 @@ def tile_two_point_leonard_stress_s2_kernel(tc, u, v, a, out):
     with ExitStack() as ctx:
         const = ctx.enter_context(tc.tile_pool(name="const", bufs=1))
         keep = ctx.enter_context(tc.tile_pool(name="keep", bufs=1))
-        raw_u = ctx.enter_context(tc.tile_pool(name="raw_u", bufs=1))
-        raw_v = ctx.enter_context(tc.tile_pool(name="raw_v", bufs=3))
-        grp_u = ctx.enter_context(tc.tile_pool(name="grp_u", bufs=3))
-        grp_v = ctx.enter_context(tc.tile_pool(name="grp_v", bufs=3))
+        raw = ctx.enter_context(tc.tile_pool(name="raw", bufs=3))
+        grp_u = ctx.enter_context(tc.tile_pool(name="grp_u", bufs=2))
+        grp_v = ctx.enter_context(tc.tile_pool(name="grp_v", bufs=4))
         sums = ctx.enter_context(tc.tile_pool(name="sums", bufs=2))
-        bars = ctx.enter_context(tc.tile_pool(name="bars", bufs=1))
-        outs = ctx.enter_context(tc.tile_pool(name="outs", bufs=4))
+        big = ctx.enter_context(tc.tile_pool(name="big", bufs=1))
         dps = ctx.enter_context(tc.psum_pool(name="dps", bufs=2))
         aps = ctx.enter_context(tc.psum_pool(name="aps", bufs=1))
         ctx.enter_context(tc.manual_schedule())
@@ -56,67 +56,77 @@ def tile_two_point_leonard_stress_s2_kernel(tc, u, v, a, out):
         ub_scales = keep.tile([P, GROUPS, M], U8, name="ub_scales", align_bytes=256)
         vb_codes = keep.tile([P, GROUPS, N], U32, name="vb_codes", align_bytes=256)
         vb_scales = keep.tile([P, GROUPS, N], U8, name="vb_scales", align_bytes=256)
-
-        u_all = raw_u.tile([P, CHUNKS, PACK, M], BF16, name="u_all", align_bytes=256)
-        v_pair = {}
-
-        def ld(kind, queue, chunk, count, c0=0, c1=N):
-            if kind == "u":
-                dst, src, cols, at = u_all, u_rows, slice(0, M), chunk
-            else:
-                pair = chunk // 2
-                if pair not in v_pair:
-                    v_pair[pair] = raw_v.tile([P, 2, PACK, N], BF16, name="v_pair", align_bytes=256)
-                dst, src, cols, at = v_pair[pair], v_rows, slice(c0, c1), chunk % 2
-            for w in (0, 1) if queue == "sp" else (2, 3):
-                first = w * R + chunk * ROWS
-                eng = nc.sync if queue == "sp" else nc.scalar
-                part = src[first : first + count * ROWS, cols]
-                to = dst[w * QUAD : (w + 1) * QUAD, at : at + count, :, cols]
-                if cols.stop - cols.start == src.shape[1]:
-                    eng.dma_start(
-                        out=to.rearrange("q c t x -> q c (t x)"),
-                        in_=part.rearrange("(c q t) x -> q c (t x)", c=count, t=PACK),
-                    )
-                else:
-                    eng.dma_start(
-                        out=to.rearrange("q c t x -> q (c t) x"),
-                        in_=part.rearrange("(q t) x -> q t x", t=PACK),
-                    )
-
-        def u_raw(c):
-            return u_all[:, c, :, :]
-
-        def v_raw(c):
-            return v_pair[c // 2][:, c % 2, :, :]
+        u_run = big.tile([P, RUN, M], BF16, name="u_run", tag="big", align_bytes=256)
+        bar_u = keep.tile([P, GROUPS, M, PACK], BF16, name="bar_u", align_bytes=256)
+        bar_v = keep.tile([P, N, PACK], BF16, name="bar_v", align_bytes=256)
+        part_b = keep.tile([P, HALF * PACK], F32, name="part_b", align_bytes=256)
 
         a_all = const.tile([P, W], BF16, name="a_all")
+        a_pos = const.tile([P, W], F32, name="a_pos")
+        a_neg = const.tile([P, W], F32, name="a_neg")
         ident = const.tile([P, P], F32, name="ident")
         warm = const.tile([P, 1], F32, name="warm")
         warm_out = const.tile([P, 1], F32, name="warm_out")
-        a_col = const.tile([P, 1], F32, name="a_col")
-        sel_v = const.tile([P, QUAD], BF16, name="sel_v")
+        diag = const.tile([P, W - 1, P], BF16, name="diag")
         sel_u = const.tile([P, QUAD], BF16, name="sel_u")
 
+        u_raw = {}
+        v_raw = {}
+        u_grp = {}
+        v_grp = {}
+        banks = {}
+        acc = {}
+        done = {}
+        res = {}
+
+        def rows(n):
+            group, w = divmod(n, W)
+            first = w * R + group * ROWS
+            return slice(first, first + ROWS)
+
+        def load_u(n):
+            u_raw[n] = raw.tile([P, PACK, M], BF16, name="u_raw", align_bytes=256)
+            nc.sync.dma_start(
+                out=u_raw[n][:].rearrange("p t i -> p (t i)"),
+                in_=u_rows[rows(n), :].rearrange("(p t) i -> p (t i)", t=PACK),
+            )
+
+        def load_v(n, h=None):
+            if h != 1:
+                v_raw[n] = raw.tile([P, PACK, N], BF16, name="v_raw", align_bytes=256)
+            if h is None:
+                nc.sync.dma_start(
+                    out=v_raw[n][:].rearrange("p t j -> p (t j)"),
+                    in_=v_rows[rows(n), :].rearrange("(p t) j -> p (t j)", t=PACK),
+                )
+            else:
+                cols = slice(h * HALF, (h + 1) * HALF)
+                nc.sync.dma_start(
+                    out=v_raw[n][:, :, cols],
+                    in_=v_rows[rows(n), cols].rearrange("(p t) j -> p t j", t=PACK),
+                )
+
+        def load_run(piece):
+            part = slice(piece * RUN // 4, (piece + 1) * RUN // 4)
+            nc.sync.dma_start(
+                out=u_run[:, part, :].rearrange("p s i -> p (s i)"),
+                in_=u_rows.rearrange("(p r) i -> p r i", r=RUN)[:, part, :].rearrange("p r i -> p (r i)"),
+            )
+
         def constants():
-            for w in range(W):
-                quad = slice(w * QUAD, (w + 1) * QUAD)
-                nc.vector.tensor_copy(out=a_col[quad, :], in_=a_all[quad, w : w + 1])
+            nc.vector.tensor_copy(out=a_pos[:], in_=a_all[:])
+            nc.vector.tensor_scalar(out=a_neg[:], in0=a_all[:], scalar1=-1.0, scalar2=None, op0=MULT)
+
+        def matrices():
+            for w in range(W - 1):
+                nc.vector.tensor_scalar(
+                    out=diag[:, w, :], in0=ident[:], scalar1=a_pos[:, w : w + 1], scalar2=None, op0=MULT
+                )
             for w in range(W):
                 quad = slice(w * QUAD, (w + 1) * QUAD)
                 nc.vector.tensor_scalar(
-                    out=sel_v[quad, :], in0=ident[quad, quad], scalar1=a_col[quad, :], scalar2=None, op0=MULT
+                    out=sel_u[quad, :], in0=ident[quad, quad], scalar1=a_neg[quad, w : w + 1], scalar2=None, op0=MULT
                 )
-            nc.vector.tensor_scalar(out=sel_u[:], in0=sel_v[:], scalar1=-1.0, scalar2=None, op0=MULT)
-
-        u_grp = {}
-        v_grp = {}
-        sum_u = {}
-        sum_v = {}
-        bar_u = {}
-        bar_v = {}
-        banks = {}
-        acc = {}
 
         def spread(dst, src):
             return (
@@ -124,106 +134,122 @@ def tile_two_point_leonard_stress_s2_kernel(tc, u, v, a, out):
                 src.rearrange("p t (c i) -> p c t i", i=4),
             )
 
-        def au(c, part):
-            if part == 0:
-                u_grp[c] = grp_u.tile([P, M, PACK], BF16, name="u_grp", align_bytes=256)
-            cols = slice(part * M // 2, (part + 1) * M // 2)
-            dst, src = spread(u_grp[c][:, cols, :], u_raw(c)[:, :, cols])
-            nc.scalar.activation(out=dst, in_=src, func=COPY, scale=a_col[:, 0:1])
+        def au(n):
+            u_grp[n] = grp_u.tile([P, M, PACK], BF16, name="u_grp", align_bytes=256)
+            dst, src = spread(u_grp[n][:], u_raw[n][:])
+            w = n % W
+            nc.scalar.activation(out=dst, in_=src, func=COPY, scale=a_pos[:, w : w + 1])
 
-        def gv(c, h):
-            g = grp_v.tile([P, HALF, PACK], BF16, name="v_grp", align_bytes=256)
-            dst, src = spread(g[:], v_raw(c)[:, :, h * HALF : (h + 1) * HALF])
-            nc.vector.tensor_copy(out=dst, in_=src)
-            v_grp[c, h] = g
+        def gv(n, h):
+            if n not in v_grp:
+                v_grp[n] = grp_v.tile([P, N, PACK], BF16, name="v_grp", align_bytes=256)
+            cols = slice(0, V_COLS) if h == 0 else slice(V_COLS, N)
+            dst, src = spread(v_grp[n][:, cols, :], v_raw[n][:, :, cols])
+            if h == 0:
+                nc.vector.tensor_copy(out=dst, in_=src)
+            else:
+                nc.scalar.copy(out=dst, in_=src)
 
-        def qu(c):
+        def flat(n, h):
+            return v_grp[n][:, h * HALF : (h + 1) * HALF, :].rearrange("p c t -> p (c t)")
+
+        def qu(n):
             nc.vector.quantize_mx(
-                out=u_codes[:, c, :].bitcast(E5),
-                scales=u_scales[:, c, :],
-                in_=u_grp[c][:].rearrange("p c t -> p (c t)"),
+                out=u_codes[:, n, :].bitcast(E5),
+                scales=u_scales[:, n, :],
+                in_=u_grp[n][:].rearrange("p c t -> p (c t)"),
             )
 
-        def qv(c, h):
+        def qv(n, h):
             cols = slice(h * HALF, (h + 1) * HALF)
             nc.vector.quantize_mx(
-                out=v_codes[:, c, cols].bitcast(E4),
-                scales=v_scales[:, c, cols],
-                in_=v_grp[c, h][:].rearrange("p c t -> p (c t)"),
+                out=v_codes[:, n, cols].bitcast(E4), scales=v_scales[:, n, cols], in_=flat(n, h)
             )
 
-        def sum_matmuls(bank, data, sel, blocks):
-            rhs = sel[:].rearrange("p (b y) -> p b y", b=4)
-            for blk in blocks:
-                for t in range(PACK):
-                    dst = bank[:, blk, t % 2, :].rearrange("j (b h y) -> j b h y", b=4, h=2)
-                    nc.tensor.matmul(
-                        out=dst[:, :, t // 2, :],
-                        lhsT=data[:, t, blk * P : (blk + 1) * P],
-                        rhs=rhs,
-                        start=True,
-                        stop=True,
-                    )
+        def bar_half(h):
+            return bar_v[:, h * HALF : (h + 1) * HALF, :].rearrange("p c t -> p (c t)")
 
-        def sv(c, part=None):
-            if part != 1:
-                banks["v", c] = dps.tile([P, NT, 2, 2 * QUAD], BF16, name="bank_sv", tag="d")
-            blocks = {None: range(NT), 0: range(NT // 2), 1: range(NT // 2, NT)}[part]
-            sum_matmuls(banks["v", c], v_raw(c), sel_v, blocks)
+        def add_b(n):
+            w = n % W
+            weight = a_pos[:, w : w + 1]
+            if w == 0:
+                nc.vector.tensor_scalar(out=part_b[:], in0=flat(n, 1), scalar1=weight, scalar2=None, op0=MULT)
+            else:
+                dst = bar_half(1) if w == W - 1 else part_b[:]
+                nc.vector.scalar_tensor_tensor(
+                    out=dst, in0=flat(n, 1), scalar=weight, in1=part_b[:], op0=MULT, op1=ADD
+                )
 
-        def su(c):
-            banks["u", c] = dps.tile([P, MT, 2, 2 * QUAD], BF16, name="bank_su", tag="d")
-            sum_matmuls(banks["u", c], u_raw(c), sel_u, range(MT))
+        def pa(group, b):
+            bank = dps.tile([P, HALF], F32, name="bank_a", tag="d")
+            for w in range(W - 1):
+                nc.tensor.matmul(
+                    out=bank[:],
+                    lhsT=diag[:, w, :],
+                    rhs=flat(W * group + w, 0)[:, b * HALF : (b + 1) * HALF],
+                    start=w == 0,
+                    stop=w == W - 2,
+                )
+            banks["a", group, b] = bank
 
-        def ks(kind, c):
-            group, slot = divmod(c, GROUP)
-            which, blocks = (sum_v, NT) if kind == "v" else (sum_u, MT)
-            if slot == 0:
-                which[group] = sums.tile([P, blocks, 2, 2 * P], BF16, name="sum_" + kind, align_bytes=64)
-            cols = slice(slot * 2 * QUAD, (slot + 1) * 2 * QUAD)
-            nc.scalar.copy(out=which[group][:, :, :, cols], in_=banks[kind, c][:])
+        def add_a(group, b):
+            part = slice(b * HALF, (b + 1) * HALF)
+            nc.vector.scalar_tensor_tensor(
+                out=bar_half(0)[:, part],
+                in0=flat(W * group + W - 1, 0)[:, part],
+                scalar=a_pos[:, W - 1 : W],
+                in1=banks["a", group, b][:],
+                op0=MULT,
+                op1=ADD,
+            )
 
-        def turn(kind, group, pair):
-            which = sum_v if kind == "v" else sum_u
-            bank = dps.tile([P, 2, 2 * P], F32, name="bank_t", tag="d")
-            for b in range(2):
+        sum_u = {}
+
+        def d1(b):
+            bank = dps.tile([P, 2, RUN // PACK, 2, QUAD], BF16, name="bank_d", tag="d")
+            for s in range(RUN):
+                nc.tensor.matmul(
+                    out=bank[:, s % PACK // 2, s // PACK, s % 2, :],
+                    lhsT=u_run[:, s, b * P : (b + 1) * P],
+                    rhs=sel_u[:],
+                    start=True,
+                    stop=True,
+                )
+            banks["d", b] = bank
+
+        def kd(b):
+            sum_u[b] = sums.tile([P, 2, GROUPS, 2 * P], BF16, name="sum_u", align_bytes=256)
+            nc.scalar.copy(
+                out=sum_u[b][:].rearrange("i h g (k x) -> i h (g k) x", k=QUAD // GROUPS),
+                in_=banks["d", b][:].rearrange("i h y e k -> i h k (y e)"),
+            )
+
+        def turn(b):
+            bank = dps.tile([P, GROUPS, 2, P], F32, name="bank_t", tag="d")
+            for group in range(GROUPS):
                 for half in range(2):
-                    nc.tensor.transpose(
-                        bank[:, half, b * P : (b + 1) * P],
-                        which[group][:, 2 * pair + b, half, :].bitcast(F32),
-                        ident[:],
-                    )
-            banks[kind, group, pair] = bank
+                    nc.tensor.transpose(bank[:, group, half, :], sum_u[b][:, half, group, :].bitcast(F32), ident[:])
+            banks["t", b] = bank
 
-        def kb(kind, group, pair, engine="s"):
-            if pair == 0 and kind == "u":
-                bar_u[group] = bars.tile([P, M, PACK], BF16, name="bar_u", align_bytes=256)
-            if pair == 0 and kind == "v":
-                bar_v[group] = bars.tile([P, N, PACK], BF16, name="bar_v", align_bytes=256)
-            bar = (bar_v if kind == "v" else bar_u)[group]
-            words = bar[:, pair * 2 * P : (pair + 1) * 2 * P, :].rearrange("p c t -> p (c t)").bitcast(F32)
-            move = nc.scalar.copy if engine == "s" else nc.vector.tensor_copy
-            move(
-                out=words.rearrange("p (c h) -> p c h", h=2),
-                in_=banks[kind, group, pair][:].rearrange("p h c -> p c h"),
+        def kt(b):
+            words = bar_u[:, :, b * P : (b + 1) * P, :].rearrange("m g c t -> m g (c t)").bitcast(F32)
+            nc.scalar.copy(
+                out=words.rearrange("m g (c h) -> m g c h", h=2),
+                in_=banks["t", b][:].rearrange("m g h c -> m g c h"),
             )
 
         def qbu(group):
             nc.vector.quantize_mx(
                 out=ub_codes[:, group, :].bitcast(E4),
                 scales=ub_scales[:, group, :],
-                in_=bar_u[group][:].rearrange("p c t -> p (c t)"),
+                in_=bar_u[:, group, :, :].rearrange("p c t -> p (c t)"),
             )
 
         def qbv(group, h):
             cols = slice(h * HALF, (h + 1) * HALF)
             nc.vector.quantize_mx(
-                out=vb_codes[:, group, cols].bitcast(E4),
-                scales=vb_scales[:, group, cols],
-                in_=bar_v[group][:, cols, :].rearrange("p c t -> p (c t)"),
+                out=vb_codes[:, group, cols].bitcast(E4), scales=vb_scales[:, group, cols], in_=bar_half(h)
             )
-
-        done = {}
 
         def mx(mt, h, kind, k):
             if kind == "main":
@@ -249,259 +275,235 @@ def tile_two_point_leonard_stress_s2_kernel(tc, u, v, a, out):
                 stop=done[key] == PASSES,
             )
 
-        res = {}
-
         def oc(mt, h, engine):
-            res[mt, h] = outs.tile([P, HALF], F32, name="res")
+            if not res:
+                stage = big.tile([P, 2 * MT, HALF], F32, name="stage", tag="big", align_bytes=256)
+                for i in range(2 * MT):
+                    res[i % MT, i // MT] = stage[:, i, :]
             if engine == "v":
-                nc.vector.tensor_copy(out=res[mt, h][:], in_=acc[mt, h][:])
+                nc.vector.tensor_copy(out=res[mt, h], in_=acc[mt, h][:])
             else:
-                nc.scalar.copy(out=res[mt, h][:], in_=acc[mt, h][:])
+                nc.scalar.copy(out=res[mt, h], in_=acc[mt, h][:])
 
         def st(mt, h):
             nc.sync.dma_start(
-                out=out[mt * P : (mt + 1) * P, h * HALF : (h + 1) * HALF], in_=res[mt, h][:]
+                out=out[mt * P : (mt + 1) * P, h * HALF : (h + 1) * HALF], in_=res[mt, h]
             )
 
         nc.sync.dma_start(out=a_all[:], in_=a.partition_broadcast(P))
-        ld("v", "act", 0, 1, 0, 512)
+        load_u(0)
+        load_v(0, 0)
+        load_v(0, 1)
+        load_v(1)
+        load_u(1)
+        load_v(2)
+        load_u(2)
         make_identity(nc, ident[:])
         nc.vector.memset(warm[:], 0.0)
-        ld("v", "sp", 0, 1, 0, 512)
-        ld("u", "act", 0, 1)
-        ld("u", "sp", 0, 1)
-        ld("v", "act", 0, 1, 512, 1024)
-        constants()
-        ld("v", "sp", 0, 1, 512, 1024)
-        ld("v", "act", 1, 1)
-        sv(0, 0)
-        gv(0, 0)
-        ld("v", "sp", 1, 1)
         nc.scalar.activation(out=warm_out[:], in_=warm[:], func=COPY)
-        ld("u", "act", 1, 1)
-        su(0)
-        ld("u", "sp", 1, 1)
-        qv(0, 0)
-        au(0, 0)
-        sv(0, 1)
+        constants()
+        au(0)
+        gv(0, 0)
+        matrices()
         gv(0, 1)
-        ld("v", "sp", 2, 1)
-        au(0, 1)
-        ld("u", "sp", 2, 2)
-        qv(0, 1)
-        ks("v", 0)
+        qv(0, 0)
         qu(0)
-        ld("v", "act", 2, 1)
-        sv(1)
-        ld("v", "sp", 3, 1)
-        gv(1, 1)
-        ks("u", 0)
-        mx(3, 0, "main", 0)
-        ld("u", "act", 2, 2)
-        mx(1, 1, "main", 0)
-        ld("v", "sp", 4, 2)
-        mx(1, 0, "main", 0)
+        load_v(3)
+        load_u(3)
+        au(1)
         gv(1, 0)
-        mx(0, 1, "main", 0)
-        su(1)
-        mx(2, 0, "main", 0)
+        gv(1, 1)
+        qv(0, 1)
         mx(0, 0, "main", 0)
-        qv(1, 1)
-        au(1, 0)
+        mx(1, 0, "main", 0)
+        mx(2, 0, "main", 0)
+        mx(3, 0, "main", 0)
+        mx(0, 1, "main", 0)
+        mx(1, 1, "main", 0)
+        add_b(0)
         qv(1, 0)
-        ld("v", "act", 3, 1)
-        gv(2, 1)
-        ld("u", "sp", 4, 4)
-        ks("u", 1)
-        gv(2, 0)
-        ks("v", 1)
-        au(1, 1)
-        sv(2)
-        ld("v", "sp", 6, 2)
-        qv(2, 1)
-        su(2)
-        qv(2, 0)
-        au(2, 0)
         qu(1)
-        ks("u", 2)
-        mx(1, 1, "main", 1)
-        ld("v", "act", 4, 2)
+        load_v(4)
+        load_u(4)
+        load_run(0)
+        load_run(1)
+        load_run(2)
+        load_run(3)
+        au(2)
+        gv(2, 0)
+        gv(2, 1)
+        qv(1, 1)
         mx(0, 0, "main", 1)
-        gv(3, 0)
-        au(3, 0)
-        mx(0, 1, "main", 1)
-        mx(3, 0, "main", 1)
         mx(1, 0, "main", 1)
-        su(3)
-        ks("v", 2)
-        gv(3, 1)
         mx(2, 0, "main", 1)
-        au(3, 1)
-        sv(3)
-        qv(3, 0)
-        ks("u", 3)
-        ks("v", 3)
-        qu(3)
-        ld("u", "act", 4, 4)
-        qv(3, 1)
-        turn("u", 0, 0)
-        au(2, 1)
-        mx(0, 0, "main", 3)
-        mx(0, 1, "main", 3)
-        mx(1, 0, "main", 3)
-        mx(1, 1, "main", 3)
-        kb("u", 0, 0)
-        mx(3, 0, "main", 3)
+        mx(3, 0, "main", 1)
+        mx(0, 1, "main", 1)
+        mx(1, 1, "main", 1)
+        add_b(1)
+        qv(2, 0)
         qu(2)
-        mx(2, 0, "main", 3)
-        ld("v", "act", 6, 2)
-        turn("u", 0, 1)
-        mx(3, 0, "main", 2)
-        gv(5, 0)
-        kb("u", 0, 1)
-        sv(4)
-        turn("v", 0, 0)
-        qbu(0)
-        ks("v", 4)
+        pa(0, 0)
+        pa(0, 1)
+        load_v(5)
+        load_u(5)
+        au(3)
+        gv(3, 0)
+        gv(3, 1)
+        qv(2, 1)
+        add_a(0, 0)
+        pa(0, 2)
+        add_a(0, 1)
+        pa(0, 3)
         mx(0, 0, "main", 2)
-        mx(0, 1, "main", 2)
-        qv(5, 0)
-        kb("v", 0, 0)
         mx(1, 0, "main", 2)
-        mx(1, 1, "main", 2)
-        gv(4, 0)
         mx(2, 0, "main", 2)
-        turn("v", 0, 1)
-        kb("v", 0, 1)
+        mx(3, 0, "main", 2)
+        mx(0, 1, "main", 2)
+        mx(1, 1, "main", 2)
+        qv(3, 0)
+        add_a(0, 2)
+        qu(3)
+        add_a(0, 3)
+        add_b(2)
+        load_v(6)
+        load_u(6)
+        au(4)
+        gv(4, 0)
         gv(4, 1)
-        turn("v", 0, 2)
-        su(4)
-        au(4, 0)
+        qv(3, 1)
+        d1(0)
+        kd(0)
+        mx(0, 0, "main", 3)
+        mx(1, 0, "main", 3)
+        mx(2, 0, "main", 3)
+        mx(3, 0, "main", 3)
+        mx(0, 1, "main", 3)
+        mx(1, 1, "main", 3)
+        add_b(3)
         qv(4, 0)
-        qv(4, 1)
-        ks("u", 4)
         qbv(0, 0)
-        kb("v", 0, 2)
-        sv(5)
-        gv(5, 1)
-        au(4, 1)
-        turn("v", 0, 3)
-        mx(1, 0, "bar", 0)
-        mx(3, 0, "bar", 0)
-        ks("v", 5)
         qu(4)
-        mx(0, 0, "bar", 0)
-        mx(2, 0, "bar", 0)
-        au(5, 0)
-        qv(5, 1)
-        su(5)
-        mx(1, 0, "main", 4)
-        mx(0, 1, "main", 4)
-        gv(6, 1)
-        ks("u", 5)
-        mx(0, 0, "main", 4)
-        kb("v", 0, 3)
-        mx(1, 1, "main", 4)
-        mx(3, 0, "main", 4)
-        au(6, 0)
-        mx(2, 0, "main", 4)
         qbv(0, 1)
-        sv(6)
-        gv(7, 0)
-        au(5, 1)
+        d1(1)
+        kd(1)
+        turn(0)
+        kt(0)
+        turn(1)
+        kt(1)
+        load_v(7)
+        load_u(7)
+        au(5)
+        gv(5, 0)
+        gv(5, 1)
+        qv(4, 1)
+        d1(2)
+        kd(2)
+        mx(0, 0, "main", 4)
+        mx(1, 0, "main", 4)
+        mx(2, 0, "main", 4)
+        mx(3, 0, "main", 4)
+        mx(0, 1, "main", 4)
+        mx(1, 1, "main", 4)
+        add_b(4)
+        qv(5, 0)
+        qu(5)
+        d1(3)
+        kd(3)
+        turn(2)
+        kt(2)
+        turn(3)
+        kt(3)
+        au(6)
+        gv(6, 0)
+        gv(6, 1)
+        qv(5, 1)
+        mx(0, 0, "main", 5)
+        mx(1, 0, "main", 5)
+        mx(2, 0, "main", 5)
+        mx(3, 0, "main", 5)
+        mx(0, 1, "main", 5)
+        mx(1, 1, "main", 5)
+        add_b(5)
+        qv(6, 0)
+        qu(6)
+        pa(1, 0)
+        pa(1, 1)
+        qbu(0)
+        qbu(1)
+        mx(0, 0, "bar", 0)
+        mx(1, 0, "bar", 0)
+        mx(2, 0, "bar", 0)
+        mx(3, 0, "bar", 0)
         mx(0, 1, "bar", 0)
         mx(1, 1, "bar", 0)
-        sv(7)
+        au(7)
+        gv(7, 0)
+        gv(7, 1)
         qv(6, 1)
-        ks("v", 6)
-        qu(5)
-        au(6, 1)
-        su(6)
-        gv(6, 0)
-        mx(2, 0, "main", 5)
-        mx(0, 1, "main", 5)
-        ks("u", 6)
-        mx(3, 0, "main", 5)
-        ks("v", 7)
-        mx(1, 1, "main", 5)
-        qu(6)
-        su(7)
-        au(7, 0)
-        mx(0, 0, "main", 5)
-        qv(6, 0)
+        add_a(1, 0)
+        pa(1, 2)
+        add_a(1, 1)
+        pa(1, 3)
+        mx(0, 0, "main", 6)
+        mx(1, 0, "main", 6)
+        mx(2, 0, "main", 6)
+        mx(3, 0, "main", 6)
         mx(0, 1, "main", 6)
         mx(1, 1, "main", 6)
         qv(7, 0)
-        ks("u", 7)
-        mx(1, 0, "main", 6)
-        au(7, 1)
-        mx(3, 0, "main", 6)
-        gv(7, 1)
-        mx(0, 0, "main", 6)
-        turn("u", 1, 0)
-        turn("u", 1, 1)
-        kb("u", 1, 0)
-        mx(2, 0, "main", 6)
+        add_a(1, 2)
+        add_a(1, 3)
+        add_b(6)
         qu(7)
-        mx(1, 0, "main", 5)
-        kb("u", 1, 1)
-        turn("v", 1, 0)
         qv(7, 1)
-        mx(2, 0, "main", 7)
-        qbu(1)
-        kb("v", 1, 0)
-        mx(1, 0, "main", 7)
-        mx(3, 0, "main", 7)
-        mx(0, 1, "main", 7)
-        turn("v", 1, 2)
-        turn("v", 1, 1)
-        kb("v", 1, 2)
-        mx(0, 0, "main", 7)
-        mx(1, 1, "main", 7)
-        kb("v", 1, 1)
-        mx(2, 1, "main", 1)
-        mx(2, 1, "bar", 0)
-        mx(2, 1, "main", 7)
-        qbv(1, 0)
-        mx(2, 1, "main", 3)
-        mx(2, 1, "main", 6)
-        mx(0, 0, "bar", 1)
-        mx(3, 0, "bar", 1)
-        mx(2, 0, "bar", 1)
-        oc(0, 0, "s")
-        turn("v", 1, 3)
-        oc(3, 0, "v")
-        oc(2, 0, "s")
-        mx(2, 1, "main", 5)
-        st(0, 0)
-        st(3, 0)
-        mx(1, 0, "bar", 1)
-        kb("v", 1, 3)
         mx(2, 1, "main", 0)
-        st(2, 0)
-        mx(2, 1, "main", 2)
-        oc(1, 0, "v")
-        mx(2, 1, "main", 4)
-        mx(3, 1, "main", 5)
-        qbv(1, 1)
-        st(1, 0)
-        mx(3, 1, "main", 4)
-        mx(3, 1, "main", 7)
-        mx(0, 1, "bar", 1)
-        mx(3, 1, "bar", 1)
-        mx(2, 1, "bar", 1)
-        oc(0, 1, "s")
-        mx(3, 1, "main", 6)
         mx(3, 1, "main", 0)
-        st(0, 1)
-        mx(1, 1, "bar", 1)
-        oc(2, 1, "s")
-        mx(3, 1, "bar", 0)
-        mx(3, 1, "main", 2)
-        oc(1, 1, "v")
-        st(2, 1)
+        mx(2, 1, "main", 1)
         mx(3, 1, "main", 1)
+        mx(2, 1, "main", 2)
+        mx(3, 1, "main", 2)
+        mx(2, 1, "main", 3)
         mx(3, 1, "main", 3)
+        mx(2, 1, "main", 4)
+        mx(3, 1, "main", 4)
+        mx(2, 1, "main", 5)
+        mx(3, 1, "main", 5)
+        mx(2, 1, "main", 6)
+        mx(3, 1, "main", 6)
+        mx(2, 1, "bar", 0)
+        mx(3, 1, "bar", 0)
+        mx(0, 0, "main", 7)
+        mx(1, 0, "main", 7)
+        mx(2, 0, "main", 7)
+        mx(3, 0, "main", 7)
+        qbv(1, 0)
+        add_b(7)
+        mx(0, 0, "bar", 1)
+        mx(1, 0, "bar", 1)
+        mx(2, 0, "bar", 1)
+        mx(3, 0, "bar", 1)
+        oc(0, 0, "s")
+        st(0, 0)
+        oc(1, 0, "s")
+        st(1, 0)
+        oc(2, 0, "s")
+        st(2, 0)
+        oc(3, 0, "s")
+        st(3, 0)
+        mx(0, 1, "main", 7)
+        mx(1, 1, "main", 7)
+        mx(2, 1, "main", 7)
+        mx(3, 1, "main", 7)
+        qbv(1, 1)
+        mx(0, 1, "bar", 1)
+        mx(1, 1, "bar", 1)
+        mx(2, 1, "bar", 1)
+        mx(3, 1, "bar", 1)
+        oc(0, 1, "v")
+        st(0, 1)
+        oc(1, 1, "s")
         st(1, 1)
-        oc(3, 1, "v")
+        oc(2, 1, "v")
+        st(2, 1)
+        oc(3, 1, "s")
         st(3, 1)

@@ -27,7 +27,6 @@ HALF = 512
 MT = M // P
 BLK = HALF // P
 PASSES = CHUNKS + GROUPS
-V_COLS = 512
 LATE = [(2, 1), (3, 1)]
 
 
@@ -84,26 +83,19 @@ def tile_two_point_leonard_stress_s2_kernel(tc, u, v, a, out):
             first = w * R + group * ROWS
             return slice(first, first + ROWS)
 
-        def load_u(n):
-            u_raw[n] = raw.tile([P, PACK, M], BF16, name="u_raw", align_bytes=256)
-            nc.sync.dma_start(
-                out=u_raw[n][:].rearrange("p t i -> p (t i)"),
-                in_=u_rows[rows(n), :].rearrange("(p t) i -> p (t i)", t=PACK),
-            )
-
-        def load_v(n, h=None):
-            if h != 1:
-                v_raw[n] = raw.tile([P, PACK, N], BF16, name="v_raw", align_bytes=256)
-            if h is None:
+        def load(n, kind, c0=0, c1=None):
+            src, held, width = (u_rows, u_raw, M) if kind == "u" else (v_rows, v_raw, N)
+            if n not in held:
+                held[n] = raw.tile([P, PACK, width], BF16, name=kind + "_raw", align_bytes=256)
+            if c1 is None:
                 nc.sync.dma_start(
-                    out=v_raw[n][:].rearrange("p t j -> p (t j)"),
-                    in_=v_rows[rows(n), :].rearrange("(p t) j -> p (t j)", t=PACK),
+                    out=held[n][:].rearrange("p t x -> p (t x)"),
+                    in_=src[rows(n), :].rearrange("(p t) x -> p (t x)", t=PACK),
                 )
             else:
-                cols = slice(h * HALF, (h + 1) * HALF)
                 nc.sync.dma_start(
-                    out=v_raw[n][:, :, cols],
-                    in_=v_rows[rows(n), cols].rearrange("(p t) j -> p t j", t=PACK),
+                    out=held[n][:, :, c0:c1],
+                    in_=src[rows(n), c0:c1].rearrange("(p t) x -> p t x", t=PACK),
                 )
 
         def load_run(piece):
@@ -134,18 +126,18 @@ def tile_two_point_leonard_stress_s2_kernel(tc, u, v, a, out):
                 src.rearrange("p t (c i) -> p c t i", i=4),
             )
 
-        def au(n):
-            u_grp[n] = grp_u.tile([P, M, PACK], BF16, name="u_grp", align_bytes=256)
-            dst, src = spread(u_grp[n][:], u_raw[n][:])
+        def au(n, c0=0, c1=M):
+            if n not in u_grp:
+                u_grp[n] = grp_u.tile([P, M, PACK], BF16, name="u_grp", align_bytes=256)
+            dst, src = spread(u_grp[n][:, c0:c1, :], u_raw[n][:, :, c0:c1])
             w = n % W
             nc.scalar.activation(out=dst, in_=src, func=COPY, scale=a_pos[:, w : w + 1])
 
-        def gv(n, h):
+        def gv(n, engine, c0, c1):
             if n not in v_grp:
                 v_grp[n] = grp_v.tile([P, N, PACK], BF16, name="v_grp", align_bytes=256)
-            cols = slice(0, V_COLS) if h == 0 else slice(V_COLS, N)
-            dst, src = spread(v_grp[n][:, cols, :], v_raw[n][:, :, cols])
-            if h == 0:
+            dst, src = spread(v_grp[n][:, c0:c1, :], v_raw[n][:, :, c0:c1])
+            if engine == "v":
                 nc.vector.tensor_copy(out=dst, in_=src)
             else:
                 nc.scalar.copy(out=dst, in_=src)
@@ -153,11 +145,11 @@ def tile_two_point_leonard_stress_s2_kernel(tc, u, v, a, out):
         def flat(n, h):
             return v_grp[n][:, h * HALF : (h + 1) * HALF, :].rearrange("p c t -> p (c t)")
 
-        def qu(n):
+        def qu(n, c0=0, c1=M):
             nc.vector.quantize_mx(
-                out=u_codes[:, n, :].bitcast(E5),
-                scales=u_scales[:, n, :],
-                in_=u_grp[n][:].rearrange("p c t -> p (c t)"),
+                out=u_codes[:, n, c0:c1].bitcast(E5),
+                scales=u_scales[:, n, c0:c1],
+                in_=u_grp[n][:, c0:c1, :].rearrange("p c t -> p (c t)"),
             )
 
         def qv(n, h):
@@ -291,143 +283,148 @@ def tile_two_point_leonard_stress_s2_kernel(tc, u, v, a, out):
             )
 
         nc.sync.dma_start(out=a_all[:], in_=a.partition_broadcast(P))
-        load_u(0)
-        load_v(0, 0)
-        load_v(0, 1)
-        load_v(1)
-        load_u(1)
-        load_v(2)
-        load_u(2)
+        load(0, "v", 0, 256)
+        load(0, "u", 0, 256)
+        load(0, "v", 256, 512)
+        load(0, "u", 256, 512)
+        load(0, "v", 512, 1024)
+        load(1, "v", 0, 512)
+        load(1, "u")
+        load(1, "v", 512, 1024)
+        load(2, "v")
+        load(2, "u")
         make_identity(nc, ident[:])
         nc.vector.memset(warm[:], 0.0)
         nc.scalar.activation(out=warm_out[:], in_=warm[:], func=COPY)
         constants()
-        au(0)
-        gv(0, 0)
+        gv(0, "v", 0, 256)
+        au(0, 0, 256)
+        gv(0, "v", 256, 512)
+        au(0, 256, 512)
         matrices()
-        gv(0, 1)
         qv(0, 0)
+        gv(0, "s", 512, 1024)
         qu(0)
-        load_v(3)
-        load_u(3)
-        au(1)
-        gv(1, 0)
-        gv(1, 1)
-        qv(0, 1)
         mx(0, 0, "main", 0)
         mx(1, 0, "main", 0)
         mx(2, 0, "main", 0)
         mx(3, 0, "main", 0)
+        load(3, "v")
+        load(3, "u")
+        gv(1, "v", 0, 512)
+        au(1)
+        qv(0, 1)
+        qv(1, 0)
+        gv(1, "s", 512, 1024)
+        add_b(0)
+        qu(1)
         mx(0, 1, "main", 0)
         mx(1, 1, "main", 0)
-        add_b(0)
-        qv(1, 0)
-        qu(1)
-        load_v(4)
-        load_u(4)
-        load_run(0)
-        load_run(1)
-        load_run(2)
-        load_run(3)
-        au(2)
-        gv(2, 0)
-        gv(2, 1)
-        qv(1, 1)
         mx(0, 0, "main", 1)
         mx(1, 0, "main", 1)
         mx(2, 0, "main", 1)
         mx(3, 0, "main", 1)
-        mx(0, 1, "main", 1)
-        mx(1, 1, "main", 1)
-        add_b(1)
-        qv(2, 0)
-        qu(2)
+        load(4, "v")
+        load(4, "u")
+        load_run(0)
+        load_run(1)
+        load_run(2)
+        load_run(3)
+        gv(2, "v", 0, 512)
+        au(2)
         pa(0, 0)
         pa(0, 1)
-        load_v(5)
-        load_u(5)
-        au(3)
-        gv(3, 0)
-        gv(3, 1)
-        qv(2, 1)
-        add_a(0, 0)
-        pa(0, 2)
-        add_a(0, 1)
-        pa(0, 3)
+        qv(1, 1)
+        qv(2, 0)
+        gv(2, "s", 512, 1024)
+        add_b(1)
+        qu(2)
+        mx(0, 1, "main", 1)
+        mx(1, 1, "main", 1)
         mx(0, 0, "main", 2)
         mx(1, 0, "main", 2)
         mx(2, 0, "main", 2)
         mx(3, 0, "main", 2)
+        load(5, "v")
+        load(5, "u")
+        gv(3, "v", 0, 512)
+        au(3)
+        qv(2, 1)
+        add_a(0, 0)
+        add_a(0, 1)
+        pa(0, 2)
+        pa(0, 3)
+        qv(3, 0)
+        gv(3, "s", 512, 1024)
+        add_b(2)
+        add_a(0, 2)
+        add_a(0, 3)
+        qu(3)
         mx(0, 1, "main", 2)
         mx(1, 1, "main", 2)
-        qv(3, 0)
-        add_a(0, 2)
-        qu(3)
-        add_a(0, 3)
-        add_b(2)
-        load_v(6)
-        load_u(6)
-        au(4)
-        gv(4, 0)
-        gv(4, 1)
-        qv(3, 1)
-        d1(0)
-        kd(0)
         mx(0, 0, "main", 3)
         mx(1, 0, "main", 3)
         mx(2, 0, "main", 3)
         mx(3, 0, "main", 3)
+        load(6, "v")
+        load(6, "u")
+        gv(4, "v", 0, 512)
+        au(4)
+        qv(3, 1)
+        qv(4, 0)
+        gv(4, "s", 512, 1024)
         mx(0, 1, "main", 3)
         mx(1, 1, "main", 3)
         add_b(3)
-        qv(4, 0)
         qbv(0, 0)
         qu(4)
         qbv(0, 1)
+        d1(0)
         d1(1)
+        kd(0)
         kd(1)
         turn(0)
-        kt(0)
         turn(1)
-        kt(1)
-        load_v(7)
-        load_u(7)
-        au(5)
-        gv(5, 0)
-        gv(5, 1)
-        qv(4, 1)
-        d1(2)
-        kd(2)
         mx(0, 0, "main", 4)
         mx(1, 0, "main", 4)
         mx(2, 0, "main", 4)
         mx(3, 0, "main", 4)
+        kt(0)
+        kt(1)
+        d1(2)
+        d1(3)
+        load(7, "v")
+        load(7, "u")
+        gv(5, "v", 0, 512)
+        au(5)
+        qv(4, 1)
+        qv(5, 0)
+        add_b(4)
+        qu(5)
         mx(0, 1, "main", 4)
         mx(1, 1, "main", 4)
-        add_b(4)
-        qv(5, 0)
-        qu(5)
-        d1(3)
-        kd(3)
-        turn(2)
-        kt(2)
-        turn(3)
-        kt(3)
-        au(6)
-        gv(6, 0)
-        gv(6, 1)
-        qv(5, 1)
         mx(0, 0, "main", 5)
         mx(1, 0, "main", 5)
         mx(2, 0, "main", 5)
         mx(3, 0, "main", 5)
-        mx(0, 1, "main", 5)
-        mx(1, 1, "main", 5)
-        add_b(5)
-        qv(6, 0)
-        qu(6)
+        kd(2)
+        kd(3)
+        turn(2)
+        turn(3)
+        kt(2)
+        kt(3)
+        gv(5, "s", 512, 1024)
+        gv(6, "v", 0, 512)
+        au(6)
         pa(1, 0)
         pa(1, 1)
+        gv(7, "v", 0, 512)
+        qv(6, 0)
+        qv(7, 0)
+        add_a(1, 0)
+        add_a(1, 1)
+        pa(1, 2)
+        pa(1, 3)
         qbu(0)
         qbu(1)
         mx(0, 0, "bar", 0)
@@ -436,26 +433,13 @@ def tile_two_point_leonard_stress_s2_kernel(tc, u, v, a, out):
         mx(3, 0, "bar", 0)
         mx(0, 1, "bar", 0)
         mx(1, 1, "bar", 0)
-        au(7)
-        gv(7, 0)
-        gv(7, 1)
-        qv(6, 1)
-        add_a(1, 0)
-        pa(1, 2)
-        add_a(1, 1)
-        pa(1, 3)
-        mx(0, 0, "main", 6)
-        mx(1, 0, "main", 6)
-        mx(2, 0, "main", 6)
-        mx(3, 0, "main", 6)
-        mx(0, 1, "main", 6)
-        mx(1, 1, "main", 6)
-        qv(7, 0)
+        qv(5, 1)
         add_a(1, 2)
         add_a(1, 3)
-        add_b(6)
-        qu(7)
-        qv(7, 1)
+        add_b(5)
+        qu(6)
+        mx(0, 1, "main", 5)
+        mx(1, 1, "main", 5)
         mx(2, 1, "main", 0)
         mx(3, 1, "main", 0)
         mx(2, 1, "main", 1)
@@ -468,20 +452,32 @@ def tile_two_point_leonard_stress_s2_kernel(tc, u, v, a, out):
         mx(3, 1, "main", 4)
         mx(2, 1, "main", 5)
         mx(3, 1, "main", 5)
-        mx(2, 1, "main", 6)
-        mx(3, 1, "main", 6)
         mx(2, 1, "bar", 0)
         mx(3, 1, "bar", 0)
-        mx(0, 0, "main", 7)
-        mx(1, 0, "main", 7)
-        mx(2, 0, "main", 7)
-        mx(3, 0, "main", 7)
+        mx(0, 0, "main", 6)
+        mx(1, 0, "main", 6)
+        mx(2, 0, "main", 6)
+        mx(3, 0, "main", 6)
+        gv(6, "s", 512, 1024)
+        qv(6, 1)
+        add_b(6)
+        mx(0, 1, "main", 6)
+        mx(1, 1, "main", 6)
+        mx(2, 1, "main", 6)
+        mx(3, 1, "main", 6)
+        gv(7, "s", 512, 1024)
+        au(7)
+        qv(7, 1)
         qbv(1, 0)
-        add_b(7)
+        qu(7)
         mx(0, 0, "bar", 1)
         mx(1, 0, "bar", 1)
         mx(2, 0, "bar", 1)
         mx(3, 0, "bar", 1)
+        mx(0, 0, "main", 7)
+        mx(1, 0, "main", 7)
+        mx(2, 0, "main", 7)
+        mx(3, 0, "main", 7)
         oc(0, 0, "s")
         st(0, 0)
         oc(1, 0, "s")
@@ -490,20 +486,21 @@ def tile_two_point_leonard_stress_s2_kernel(tc, u, v, a, out):
         st(2, 0)
         oc(3, 0, "s")
         st(3, 0)
+        add_b(7)
         mx(0, 1, "main", 7)
         mx(1, 1, "main", 7)
         mx(2, 1, "main", 7)
         mx(3, 1, "main", 7)
         qbv(1, 1)
         mx(0, 1, "bar", 1)
-        mx(1, 1, "bar", 1)
-        mx(2, 1, "bar", 1)
-        mx(3, 1, "bar", 1)
         oc(0, 1, "v")
         st(0, 1)
+        mx(1, 1, "bar", 1)
         oc(1, 1, "s")
         st(1, 1)
+        mx(2, 1, "bar", 1)
         oc(2, 1, "v")
         st(2, 1)
+        mx(3, 1, "bar", 1)
         oc(3, 1, "s")
         st(3, 1)

from contextlib import ExitStack

import concourse.mybir as mybir
from concourse.masks import make_identity

W, R, M, N = 4, 1024, 512, 1024
FLOPS = 2 * W * R * M * N + 2 * R * M * N

F32 = mybir.dt.float32
BF16 = mybir.dt.bfloat16
U32 = mybir.dt.uint32
U8 = mybir.dt.uint8
E4 = mybir.dt.float8_e4m3fn_x4
E5 = mybir.dt.float8_e5m2_x4
COPY = mybir.ActivationFunctionType.Copy
MULT = mybir.AluOpType.mult
ADD = mybir.AluOpType.add

P = 128
PACK = 4
ROWS = P * PACK
GROUPS = R // ROWS
CHUNKS = W * GROUPS
QUAD = P // W
RUN = W * R // P
HALF = 512
MT = M // P
BLK = HALF // P
PASSES = CHUNKS + GROUPS
LATE = [(2, 1), (3, 1)]


def tile_two_point_leonard_stress_s2_kernel(tc, u, v, a, out):
    nc = tc.nc
    u_rows = u.rearrange("w r i -> (w r) i")
    v_rows = v.rearrange("w r j -> (w r) j")

    with ExitStack() as ctx:
        const = ctx.enter_context(tc.tile_pool(name="const", bufs=1))
        keep = ctx.enter_context(tc.tile_pool(name="keep", bufs=1))
        raw = ctx.enter_context(tc.tile_pool(name="raw", bufs=3))
        grp_u = ctx.enter_context(tc.tile_pool(name="grp_u", bufs=2))
        grp_v = ctx.enter_context(tc.tile_pool(name="grp_v", bufs=4))
        sums = ctx.enter_context(tc.tile_pool(name="sums", bufs=2))
        big = ctx.enter_context(tc.tile_pool(name="big", bufs=1))
        dps = ctx.enter_context(tc.psum_pool(name="dps", bufs=2))
        aps = ctx.enter_context(tc.psum_pool(name="aps", bufs=1))
        ctx.enter_context(tc.manual_schedule())

        u_codes = keep.tile([P, CHUNKS, M], U32, name="u_codes", align_bytes=256)
        u_scales = keep.tile([P, CHUNKS, M], U8, name="u_scales", align_bytes=256)
        v_codes = keep.tile([P, CHUNKS, N], U32, name="v_codes", align_bytes=256)
        v_scales = keep.tile([P, CHUNKS, N], U8, name="v_scales", align_bytes=256)
        ub_codes = keep.tile([P, GROUPS, M], U32, name="ub_codes", align_bytes=256)
        ub_scales = keep.tile([P, GROUPS, M], U8, name="ub_scales", align_bytes=256)
        vb_codes = keep.tile([P, GROUPS, N], U32, name="vb_codes", align_bytes=256)
        vb_scales = keep.tile([P, GROUPS, N], U8, name="vb_scales", align_bytes=256)
        u_run = big.tile([P, RUN, M], BF16, name="u_run", tag="big", align_bytes=256)
        bar_u = keep.tile([P, GROUPS, M, PACK], BF16, name="bar_u", align_bytes=256)
        bar_v = keep.tile([P, N, PACK], BF16, name="bar_v", align_bytes=256)
        part_b = keep.tile([P, HALF * PACK], F32, name="part_b", align_bytes=256)

        a_all = const.tile([P, W], BF16, name="a_all")
        a_pos = const.tile([P, W], F32, name="a_pos")
        a_neg = const.tile([P, W], F32, name="a_neg")
        ident = const.tile([P, P], F32, name="ident")
        warm = const.tile([P, 1], F32, name="warm")
        warm_out = const.tile([P, 1], F32, name="warm_out")
        diag = const.tile([P, W - 1, P], BF16, name="diag")
        sel_u = const.tile([P, QUAD], BF16, name="sel_u")

        u_raw = {}
        v_raw = {}
        u_grp = {}
        v_grp = {}
        banks = {}
        acc = {}
        done = {}
        res = {}

        def rows(n):
            group, w = divmod(n, W)
            first = w * R + group * ROWS
            return slice(first, first + ROWS)

        def load(n, kind, c0=0, c1=None):
            src, held, width = (u_rows, u_raw, M) if kind == "u" else (v_rows, v_raw, N)
            if n not in held:
                held[n] = raw.tile([P, PACK, width], BF16, name=kind + "_raw", align_bytes=256)
            if c1 is None:
                nc.sync.dma_start(
                    out=held[n][:].rearrange("p t x -> p (t x)"),
                    in_=src[rows(n), :].rearrange("(p t) x -> p (t x)", t=PACK),
                )
            else:
                nc.sync.dma_start(
                    out=held[n][:, :, c0:c1],
                    in_=src[rows(n), c0:c1].rearrange("(p t) x -> p t x", t=PACK),
                )

        def load_run(piece):
            part = slice(piece * RUN // 4, (piece + 1) * RUN // 4)
            nc.sync.dma_start(
                out=u_run[:, part, :].rearrange("p s i -> p (s i)"),
                in_=u_rows.rearrange("(p r) i -> p r i", r=RUN)[:, part, :].rearrange("p r i -> p (r i)"),
            )

        def constants():
            nc.vector.tensor_copy(out=a_pos[:], in_=a_all[:])
            nc.vector.tensor_scalar(out=a_neg[:], in0=a_all[:], scalar1=-1.0, scalar2=None, op0=MULT)

        def matrices():
            for w in range(W - 1):
                nc.vector.tensor_scalar(
                    out=diag[:, w, :], in0=ident[:], scalar1=a_pos[:, w : w + 1], scalar2=None, op0=MULT
                )
            for w in range(W):
                quad = slice(w * QUAD, (w + 1) * QUAD)
                nc.vector.tensor_scalar(
                    out=sel_u[quad, :], in0=ident[quad, quad], scalar1=a_neg[quad, w : w + 1], scalar2=None, op0=MULT
                )

        def spread(dst, src):
            return (
                dst.rearrange("p (c i) t -> p c t i", i=4),
                src.rearrange("p t (c i) -> p c t i", i=4),
            )

        def au(n, c0=0, c1=M):
            if n not in u_grp:
                u_grp[n] = grp_u.tile([P, M, PACK], BF16, name="u_grp", align_bytes=256)
            dst, src = spread(u_grp[n][:, c0:c1, :], u_raw[n][:, :, c0:c1])
            w = n % W
            nc.scalar.activation(out=dst, in_=src, func=COPY, scale=a_pos[:, w : w + 1])

        def gv(n, engine, c0, c1):
            if n not in v_grp:
                v_grp[n] = grp_v.tile([P, N, PACK], BF16, name="v_grp", align_bytes=256)
            dst, src = spread(v_grp[n][:, c0:c1, :], v_raw[n][:, :, c0:c1])
            if engine == "v":
                nc.vector.tensor_copy(out=dst, in_=src)
            else:
                nc.scalar.copy(out=dst, in_=src)

        def flat(n, h):
            return v_grp[n][:, h * HALF : (h + 1) * HALF, :].rearrange("p c t -> p (c t)")

        def qu(n, c0=0, c1=M):
            nc.vector.quantize_mx(
                out=u_codes[:, n, c0:c1].bitcast(E5),
                scales=u_scales[:, n, c0:c1],
                in_=u_grp[n][:, c0:c1, :].rearrange("p c t -> p (c t)"),
            )

        def qv(n, h):
            cols = slice(h * HALF, (h + 1) * HALF)
            nc.vector.quantize_mx(
                out=v_codes[:, n, cols].bitcast(E4), scales=v_scales[:, n, cols], in_=flat(n, h)
            )

        def bar_half(h):
            return bar_v[:, h * HALF : (h + 1) * HALF, :].rearrange("p c t -> p (c t)")

        def add_b(n):
            w = n % W
            weight = a_pos[:, w : w + 1]
            if w == 0:
                nc.vector.tensor_scalar(out=part_b[:], in0=flat(n, 1), scalar1=weight, scalar2=None, op0=MULT)
            else:
                dst = bar_half(1) if w == W - 1 else part_b[:]
                nc.vector.scalar_tensor_tensor(
                    out=dst, in0=flat(n, 1), scalar=weight, in1=part_b[:], op0=MULT, op1=ADD
                )

        def pa(group, b):
            bank = dps.tile([P, HALF], F32, name="bank_a", tag="d")
            for w in range(W - 1):
                nc.tensor.matmul(
                    out=bank[:],
                    lhsT=diag[:, w, :],
                    rhs=flat(W * group + w, 0)[:, b * HALF : (b + 1) * HALF],
                    start=w == 0,
                    stop=w == W - 2,
                )
            banks["a", group, b] = bank

        def add_a(group, b):
            part = slice(b * HALF, (b + 1) * HALF)
            nc.vector.scalar_tensor_tensor(
                out=bar_half(0)[:, part],
                in0=flat(W * group + W - 1, 0)[:, part],
                scalar=a_pos[:, W - 1 : W],
                in1=banks["a", group, b][:],
                op0=MULT,
                op1=ADD,
            )

        sum_u = {}

        def d1(b):
            bank = dps.tile([P, 2, RUN // PACK, 2, QUAD], BF16, name="bank_d", tag="d")
            for s in range(RUN):
                nc.tensor.matmul(
                    out=bank[:, s % PACK // 2, s // PACK, s % 2, :],
                    lhsT=u_run[:, s, b * P : (b + 1) * P],
                    rhs=sel_u[:],
                    start=True,
                    stop=True,
                )
            banks["d", b] = bank

        def kd(b):
            sum_u[b] = sums.tile([P, 2, GROUPS, 2 * P], BF16, name="sum_u", align_bytes=256)
            nc.scalar.copy(
                out=sum_u[b][:].rearrange("i h g (k x) -> i h (g k) x", k=QUAD // GROUPS),
                in_=banks["d", b][:].rearrange("i h y e k -> i h k (y e)"),
            )

        def turn(b):
            bank = dps.tile([P, GROUPS, 2, P], F32, name="bank_t", tag="d")
            for group in range(GROUPS):
                for half in range(2):
                    nc.tensor.transpose(bank[:, group, half, :], sum_u[b][:, half, group, :].bitcast(F32), ident[:])
            banks["t", b] = bank

        def kt(b):
            words = bar_u[:, :, b * P : (b + 1) * P, :].rearrange("m g c t -> m g (c t)").bitcast(F32)
            nc.scalar.copy(
                out=words.rearrange("m g (c h) -> m g c h", h=2),
                in_=banks["t", b][:].rearrange("m g h c -> m g c h"),
            )

        def qbu(group):
            nc.vector.quantize_mx(
                out=ub_codes[:, group, :].bitcast(E4),
                scales=ub_scales[:, group, :],
                in_=bar_u[:, group, :, :].rearrange("p c t -> p (c t)"),
            )

        def qbv(group, h):
            cols = slice(h * HALF, (h + 1) * HALF)
            nc.vector.quantize_mx(
                out=vb_codes[:, group, cols].bitcast(E4), scales=vb_scales[:, group, cols], in_=bar_half(h)
            )

        def mx(mt, h, kind, k):
            if kind == "main":
                lc, ls, lt, rc, rs = u_codes, u_scales, E5, v_codes, v_scales
            else:
                lc, ls, lt, rc, rs = ub_codes, ub_scales, E4, vb_codes, vb_scales
            key = (mt, h)
            if key not in acc:
                if key in LATE:
                    acc[key] = dps.tile([P, HALF], F32, name="acc_late", tag="d")
                else:
                    acc[key] = aps.tile([P, HALF], F32, name="acc%d" % (mt + MT * h))
            ms = slice(mt * P, (mt + 1) * P)
            ns = slice(h * HALF, (h + 1) * HALF)
            done[key] = done.get(key, 0) + 1
            nc.tensor.matmul_mx(
                out=acc[key][:],
                lhsT=lc[:, k, ms].bitcast(lt),
                lhsT_scale=ls[:, k, ms],
                rhs=rc[:, k, ns].bitcast(E4),
                rhs_scale=rs[:, k, ns],
                start=done[key] == 1,
                stop=done[key] == PASSES,
            )

        def oc(mt, h, engine):
            if not res:
                stage = big.tile([P, 2 * MT, HALF], F32, name="stage", tag="big", align_bytes=256)
                for i in range(2 * MT):
                    res[i % MT, i // MT] = stage[:, i, :]
            if engine == "v":
                nc.vector.tensor_copy(out=res[mt, h], in_=acc[mt, h][:])
            else:
                nc.scalar.copy(out=res[mt, h], in_=acc[mt, h][:])

        def st(mt, h):
            nc.sync.dma_start(
                out=out[mt * P : (mt + 1) * P, h * HALF : (h + 1) * HALF], in_=res[mt, h]
            )

        nc.sync.dma_start(out=a_all[:], in_=a.partition_broadcast(P))
        load(0, "v", 0, 256)
        load(0, "u", 0, 256)
        load(0, "v", 256, 512)
        load(0, "u", 256, 512)
        load(0, "v", 512, 1024)
        load(1, "v", 0, 512)
        load(1, "u")
        load(1, "v", 512, 1024)
        load(2, "v")
        load(2, "u")
        make_identity(nc, ident[:])
        nc.vector.memset(warm[:], 0.0)
        nc.scalar.activation(out=warm_out[:], in_=warm[:], func=COPY)
        constants()
        gv(0, "v", 0, 256)
        au(0, 0, 256)
        gv(0, "v", 256, 512)
        au(0, 256, 512)
        matrices()
        qv(0, 0)
        gv(0, "s", 512, 1024)
        qu(0)
        mx(0, 0, "main", 0)
        mx(1, 0, "main", 0)
        mx(2, 0, "main", 0)
        mx(3, 0, "main", 0)
        load(3, "v")
        load(3, "u")
        gv(1, "v", 0, 512)
        au(1)
        qv(0, 1)
        qv(1, 0)
        gv(1, "s", 512, 1024)
        add_b(0)
        qu(1)
        mx(0, 1, "main", 0)
        mx(1, 1, "main", 0)
        mx(0, 0, "main", 1)
        mx(1, 0, "main", 1)
        mx(2, 0, "main", 1)
        mx(3, 0, "main", 1)
        load(4, "v")
        load(4, "u")
        load_run(0)
        load_run(1)
        load_run(2)
        load_run(3)
        gv(2, "v", 0, 512)
        au(2)
        pa(0, 0)
        pa(0, 1)
        qv(1, 1)
        qv(2, 0)
        gv(2, "s", 512, 1024)
        add_b(1)
        qu(2)
        mx(0, 1, "main", 1)
        mx(1, 1, "main", 1)
        mx(0, 0, "main", 2)
        mx(1, 0, "main", 2)
        mx(2, 0, "main", 2)
        mx(3, 0, "main", 2)
        load(5, "v")
        load(5, "u")
        gv(3, "v", 0, 512)
        au(3)
        qv(2, 1)
        add_a(0, 0)
        add_a(0, 1)
        pa(0, 2)
        pa(0, 3)
        qv(3, 0)
        gv(3, "s", 512, 1024)
        add_b(2)
        add_a(0, 2)
        add_a(0, 3)
        qu(3)
        mx(0, 1, "main", 2)
        mx(1, 1, "main", 2)
        mx(0, 0, "main", 3)
        mx(1, 0, "main", 3)
        mx(2, 0, "main", 3)
        mx(3, 0, "main", 3)
        load(6, "v")
        load(6, "u")
        gv(4, "v", 0, 512)
        au(4)
        qv(3, 1)
        qv(4, 0)
        gv(4, "s", 512, 1024)
        mx(0, 1, "main", 3)
        mx(1, 1, "main", 3)
        add_b(3)
        qbv(0, 0)
        qu(4)
        qbv(0, 1)
        d1(0)
        d1(1)
        kd(0)
        kd(1)
        turn(0)
        turn(1)
        mx(0, 0, "main", 4)
        mx(1, 0, "main", 4)
        mx(2, 0, "main", 4)
        mx(3, 0, "main", 4)
        kt(0)
        kt(1)
        d1(2)
        d1(3)
        load(7, "v")
        load(7, "u")
        gv(5, "v", 0, 512)
        au(5)
        qv(4, 1)
        qv(5, 0)
        add_b(4)
        qu(5)
        mx(0, 1, "main", 4)
        mx(1, 1, "main", 4)
        mx(0, 0, "main", 5)
        mx(1, 0, "main", 5)
        mx(2, 0, "main", 5)
        mx(3, 0, "main", 5)
        kd(2)
        kd(3)
        turn(2)
        turn(3)
        kt(2)
        kt(3)
        gv(5, "s", 512, 1024)
        gv(6, "v", 0, 512)
        au(6)
        pa(1, 0)
        pa(1, 1)
        gv(7, "v", 0, 512)
        qv(6, 0)
        qv(7, 0)
        add_a(1, 0)
        add_a(1, 1)
        pa(1, 2)
        pa(1, 3)
        qbu(0)
        qbu(1)
        mx(0, 0, "bar", 0)
        mx(1, 0, "bar", 0)
        mx(2, 0, "bar", 0)
        mx(3, 0, "bar", 0)
        mx(0, 1, "bar", 0)
        mx(1, 1, "bar", 0)
        qv(5, 1)
        add_a(1, 2)
        add_a(1, 3)
        add_b(5)
        qu(6)
        mx(0, 1, "main", 5)
        mx(1, 1, "main", 5)
        mx(2, 1, "main", 0)
        mx(3, 1, "main", 0)
        mx(2, 1, "main", 1)
        mx(3, 1, "main", 1)
        mx(2, 1, "main", 2)
        mx(3, 1, "main", 2)
        mx(2, 1, "main", 3)
        mx(3, 1, "main", 3)
        mx(2, 1, "main", 4)
        mx(3, 1, "main", 4)
        mx(2, 1, "main", 5)
        mx(3, 1, "main", 5)
        mx(2, 1, "bar", 0)
        mx(3, 1, "bar", 0)
        mx(0, 0, "main", 6)
        mx(1, 0, "main", 6)
        mx(2, 0, "main", 6)
        mx(3, 0, "main", 6)
        gv(6, "s", 512, 1024)
        qv(6, 1)
        add_b(6)
        mx(0, 1, "main", 6)
        mx(1, 1, "main", 6)
        mx(2, 1, "main", 6)
        mx(3, 1, "main", 6)
        gv(7, "s", 512, 1024)
        au(7)
        qv(7, 1)
        qbv(1, 0)
        qu(7)
        mx(0, 0, "bar", 1)
        mx(1, 0, "bar", 1)
        mx(2, 0, "bar", 1)
        mx(3, 0, "bar", 1)
        mx(0, 0, "main", 7)
        mx(1, 0, "main", 7)
        mx(2, 0, "main", 7)
        mx(3, 0, "main", 7)
        oc(0, 0, "s")
        st(0, 0)
        oc(1, 0, "s")
        st(1, 0)
        oc(2, 0, "s")
        st(2, 0)
        oc(3, 0, "s")
        st(3, 0)
        add_b(7)
        mx(0, 1, "main", 7)
        mx(1, 1, "main", 7)
        mx(2, 1, "main", 7)
        mx(3, 1, "main", 7)
        qbv(1, 1)
        mx(0, 1, "bar", 1)
        oc(0, 1, "v")
        st(0, 1)
        mx(1, 1, "bar", 1)
        oc(1, 1, "s")
        st(1, 1)
        mx(2, 1, "bar", 1)
        oc(2, 1, "v")
        st(2, 1)
        mx(3, 1, "bar", 1)
        oc(3, 1, "s")
        st(3, 1)
